import numpy as np
import ml_dtypes


def mxq(x, axis, fmt="e4m3"):
    dtype, down = {"e4m3": (ml_dtypes.float8_e4m3fn, 7), "e5m2": (ml_dtypes.float8_e5m2, 14)}[fmt]
    v = np.moveaxis(np.asarray(x, np.float32).astype(ml_dtypes.bfloat16).astype(np.float64), axis, -1)
    blocks = v.reshape(v.shape[:-1] + (-1, 32))
    amax = np.abs(blocks).max(-1, keepdims=True)
    byte = np.maximum(np.where(amax > 0, np.frexp(amax)[1] - 1 + 127, 0) - down, 1)
    scale = np.exp2(byte - 127.0)
    codes = (blocks / scale).astype(np.float32).astype(dtype).astype(np.float64)
    return np.moveaxis((codes * scale).reshape(v.shape), -1, axis)


WIDE = False


def mx_kscale(k):
    if not WIDE:
        return np.ones(k)
    levels = np.array([24, -24, 12, -12, 0])
    if k % 512:
        return np.exp2(np.random.permutation(np.resize(levels, k // 32))).repeat(32)
    a = np.empty((k // 512, 16))
    for p in range(k // 512):
        a[p, :8] = np.random.permutation(np.resize(levels, 8))
        for g in range(8):
            far = levels[np.abs(levels - a[p, g]) >= 10]
            a[p, g + 8] = far[np.random.randint(len(far))]
    return np.exp2(a.ravel()).repeat(32)


def f64(x):
    return np.asarray(x).astype(np.float64)


def striped(idx):
    return np.tile(idx.reshape(-1, 16).T, (8, 1)).astype(np.uint16)


def unstriped(offs):
    return offs[:16].T.reshape(-1).astype(np.int64)


E2M1 = np.array([0.0, 0.5, 1.0, 1.5, 2.0, 3.0, 4.0, 6.0, -0.0, -0.5, -1.0, -1.5, -2.0, -3.0, -4.0, -6.0])


def pack_weight(w, fmt):
    k, n = w.shape
    w = f64(np.asarray(w, np.float32).astype(ml_dtypes.bfloat16)).reshape(k // 32, 32, n)
    amax = np.abs(w).max(1)
    if fmt == "e4m3":
        byte = np.frexp(amax)[1] - 1 + 127 - 7
    else:
        mant, ex = np.frexp(amax / 6.0)
        byte = np.where(mant > 0.5, ex, ex - 1) + 127
    byte = np.clip(np.where(amax > 0, byte, 1), 1, 254)
    scaled = (w * np.exp2(127.0 - byte)[:, None, :]).reshape(k, n).astype(np.float32)
    by_word = np.ascontiguousarray(scaled.reshape(k // 512, 128, 4, n).transpose(0, 1, 3, 2))
    if fmt == "e4m3":
        words = by_word.astype(ml_dtypes.float8_e4m3fn).view(np.uint8)
    else:
        c = by_word.astype(ml_dtypes.float4_e2m1fn).view(np.uint8) & 0xF
        words = (c[..., 0::2] | (c[..., 1::2] << 4)).reshape(k // 512, 128, 2 * n)
    return np.ascontiguousarray(words), np.ascontiguousarray(byte.astype(np.uint8).reshape(k // 512, 16, n))


def unpack_weight(words, scales, fmt):
    g, _, n = scales.shape
    words = np.ascontiguousarray(words).reshape(g, 128, n, -1)
    if fmt == "e4m3":
        vals = words.view(ml_dtypes.float8_e4m3fn).astype(np.float64)
    else:
        nib = np.empty((g, 128, n, 4), np.uint8)
        nib[..., 0::2] = words & 0xF
        nib[..., 1::2] = words >> 4
        vals = E2M1[nib]
    vals = vals * np.repeat(np.exp2(scales.astype(np.float64) - 127.0), 8, axis=1)[..., None]
    return vals.transpose(0, 1, 3, 2).reshape(g * 512, n)


def pack_table4(v):
    words, scales = pack_weight(v, "e2m1")
    g, t = words.shape[0] // 2, v.shape[1]
    return np.ascontiguousarray(words.reshape(g, 2, 128, t, 2).transpose(0, 2, 3, 1, 4).reshape(g, 128, t, 4)), scales


def unpack_table4(words, scales):
    g, _, t, _ = words.shape
    return unpack_weight(words.reshape(g, 128, t, 2, 2).transpose(0, 3, 1, 2, 4).reshape(2 * g, 128, 2 * t), scales, "e2m1")


K, R, N, T, J = 1024, 512, 256, 2048, 512


def setup_inputs():
    n = np.random.standard_normal
    s = mx_kscale(K)[:, None]
    u = mx_kscale(R)[:, None]
    p_tab = pack_table4(n((K, T)) * s)
    p_wc = pack_weight(n((K, R)) / np.sqrt(K) / s * u.T, "e2m1")
    p_wd = pack_weight(n((R, N)) / np.sqrt(R) / u, "e2m1")
    return {
        "tab_words": p_tab[0],
        "tab_scales": p_tab[1],
        "c": (n((K, J)) * s).astype(np.float32),
        "w": (n((K, R)) / np.sqrt(K) / s * u.T).astype(np.float32),
        "wc_words": p_wc[0],
        "wc_scales": p_wc[1],
        "wd_words": p_wd[0],
        "wd_scales": p_wd[1],
        "b": (0.3 * n(N)).astype(np.float32),
        "offs": striped(np.concatenate([np.random.permutation(T)[:J] for _ in range(2)])),
    }


def reference(tab_words, tab_scales, c, w, wc_words, wc_scales, wd_words, wd_scales, b, offs):
    idx = unstriped(offs).reshape(2, J)
    tab_ = unpack_table4(tab_words, tab_scales)[:, idx]
    c_ = mxq(f64(c), 0, "e4m3")
    w_ = mxq(f64(w), 0, "e4m3")
    a0 = w_.T @ tab_[:, 0]
    a1 = w_.T @ tab_[:, 1]
    wc_ = unpack_weight(wc_words, wc_scales, "e2m1")
    ac = wc_.T @ c_
    h = np.maximum(np.maximum(a0, a1) + ac, 0.0)
    h_ = mxq(h, 0, "e4m3")
    wd_ = unpack_weight(wd_words, wd_scales, "e2m1")
    y = wd_.T @ h_
    return y + f64(b)[:, None]

@@ -1,0 +1,275 @@
+from contextlib import ExitStack
+
+import concourse.mybir as mybir
+
+K, R, N, T, J = 1024, 512, 256, 2048, 512
+FLOPS = 2 * (3 * K * R * J + R * N * J)
+
+F32 = mybir.dt.float32
+BF16 = mybir.dt.bfloat16
+I32 = mybir.dt.int32
+U32 = mybir.dt.uint32
+U16 = mybir.dt.uint16
+U8 = mybir.dt.uint8
+FP8X4 = mybir.dt.float8_e4m3fn_x4
+FP4X4 = mybir.dt.float4_e2m1fn_x4
+ALU = mybir.AluOpType
+ACT = mybir.ActivationFunctionType
+
+P = 128
+PACK = 4
+PASSES = K // (P * PACK)
+LOOKS = 2
+CHUNK = 128
+CHUNKS = J // CHUNK
+HALF = 256
+
+
+def tile_list_pnet_bias_kernel(
+    tc, tab_words, tab_scales, c, w, wc_words, wc_scales, wd_words, wd_scales, b, offs, out
+):
+    nc = tc.nc
+    with ExitStack() as ctx:
+        keep = ctx.enter_context(tc.tile_pool(name="keep", bufs=1))
+        ring = ctx.enter_context(tc.tile_pool(name="ring", bufs=4))
+        psum = ctx.enter_context(tc.psum_pool(name="psum", bufs=1))
+
+        def held(shape, dtype, name):
+            return keep.tile(shape, dtype, name=name, align_bytes=64)
+
+        offsets = keep.tile([P, LOOKS * J // 16], U16, name="offsets")
+        nc.sync.dma_start(offsets[:], offs)
+
+        tab_rows = held([P, T], U8, "tab_rows")
+        nc.sync.dma_start(
+            out=tab_rows[0:32, :].bitcast(I32), in_=tab_scales.bitcast(I32).rearrange("a q t -> q a t")
+        )
+        wc_raw = held([P, PASSES, 2 * R], U8, "wc_raw")
+        nc.sync.dma_start(
+            out=wc_raw[:].bitcast(I32), in_=wc_words.bitcast(I32).rearrange("a p n -> p a n")
+        )
+        table = held([P, T], I32, "table")
+        nc.sync.dma_start(
+            out=table[:], in_=tab_words[0].rearrange("p t b -> p (t b)").bitcast(I32)
+        )
+        wc_plane = held([P, PASSES, R], U8, "wc_plane")
+        wd_plane = held([P, N], U8, "wd_plane")
+        look_plane = held([P, PASSES, LOOKS * J], U8, "look_plane")
+        nc.gpsimd.memset(wc_plane[:].rearrange("p a r -> p (a r)").bitcast(I32), 0)
+        nc.gpsimd.memset(tab_rows[32:64, :].bitcast(I32), 0)
+        nc.vector.memset(tab_rows[64:128, :].bitcast(I32), 0)
+        nc.vector.memset(look_plane[:].rearrange("p a j -> p (a j)").bitcast(I32), 0)
+        nc.gpsimd.memset(wd_plane[:].bitcast(I32), 0)
+
+        def load_rows(src, a, h, name):
+            raw = held([P, PACK, HALF], F32, name)
+            rows = src[512 * a : 512 * (a + 1), HALF * h : HALF * (h + 1)]
+            nc.sync.dma_start(out=raw[:], in_=rows.rearrange("(p i) n -> p i n", i=PACK))
+            return raw
+
+        w_raw = {}
+        w_raw[0, 0] = load_rows(w, 0, 0, "w_raw00")
+        for q in range(4):
+            nc.sync.dma_start(
+                out=wc_plane[32 * q : 32 * q + 4, :, :].bitcast(I32),
+                in_=wc_scales[:, 4 * q : 4 * q + 4, :].bitcast(I32).rearrange("a r n -> r a n"),
+            )
+        w_raw[0, 1] = load_rows(w, 0, 1, "w_raw01")
+        w_raw[1, 0] = load_rows(w, 1, 0, "w_raw10")
+
+        picked_rows = held([P, LOOKS * J], U8, "picked_rows")
+        nc.vector.tensor_copy(out=picked_rows[:], in_=tab_rows[:].indirect(offsets[:]))
+        for q in range(4):
+            nc.sync.dma_start(
+                out=look_plane[32 * q : 32 * q + 4, :, :].bitcast(I32),
+                in_=picked_rows[8 * q : 8 * q + 8, :].bitcast(I32),
+            )
+
+        w_raw[1, 1] = load_rows(w, 1, 1, "w_raw11")
+        c_raw = {}
+        c_raw[0, 0] = load_rows(c, 0, 0, "c_raw00")
+        c_raw[1, 0] = load_rows(c, 1, 0, "c_raw10")
+        c_raw[0, 1] = load_rows(c, 0, 1, "c_raw01")
+        c_raw[1, 1] = load_rows(c, 1, 1, "c_raw11")
+        wd_raw = held([P, 2 * N], U8, "wd_raw")
+        nc.sync.dma_start(out=wd_raw[:].bitcast(I32), in_=wd_words[0].bitcast(I32))
+        for q in range(4):
+            nc.sync.dma_start(
+                out=wd_plane[32 * q : 32 * q + 4, :].bitcast(I32),
+                in_=wd_scales[0, 4 * q : 4 * q + 4, :].bitcast(I32),
+            )
+        bias = held([P, N // P], F32, "bias")
+        with nc.allow_non_contiguous_dma(reason="one bias value a partition"):
+            nc.sync.dma_start(out=bias[:], in_=b.rearrange("(s p) -> p s", p=P))
+
+        w_bf = [held([P, PACK * R], BF16, "w_bf%d" % a) for a in range(PASSES)]
+        w_codes = [held([P, R], U32, "w_codes%d" % a) for a in range(PASSES)]
+        w_plane = [held([P, R], U8, "w_plane%d" % a) for a in range(PASSES)]
+
+        def cast_w(a, h, on_vector):
+            dst = w_bf[a][:].rearrange("p (t m i) -> p m i t", t=PACK, i=PACK)[:, 64 * h : 64 * (h + 1), :, :]
+            src = w_raw[a, h][:].rearrange("p i (m t) -> p m i t", t=PACK)
+            if on_vector:
+                nc.vector.tensor_copy(out=dst, in_=src)
+            else:
+                nc.scalar.copy(out=dst, in_=src)
+
+        def quant(codes, plane, src):
+            nc.vector.quantize_mx(out=codes.bitcast(FP8X4), scales=plane, in_=src)
+
+        cast_w(0, 0, False)
+
+        look_words = []
+        for g in range(LOOKS):
+            picked = held([P, J], U32, "picked%d" % g)
+            nc.vector.tensor_copy(
+                out=picked[:],
+                in_=table[:].bitcast(U32).indirect(offsets[:, g * J // 16 : (g + 1) * J // 16]),
+            )
+            parted = held([P, PASSES, 2 * J], U8, "parted%d" % g)
+            nc.vector.tensor_copy(
+                out=parted[:].bitcast(U16),
+                in_=picked[:].bitcast(U16).rearrange("p (j d) -> p d j", d=PASSES),
+            )
+            look_words.append(parted)
+
+        cast_w(0, 1, False)
+        quant(w_codes[0][:], w_plane[0][:], w_bf[0][:])
+        wc_perm = held([P, PASSES, 2 * R], U8, "wc_perm")
+        wc_plane_perm = held([P, PASSES, R], U8, "wc_plane_perm")
+        nc.vector.tensor_copy(
+            out=wc_perm[:].bitcast(U16).rearrange("p a (t m) -> p a m t", t=PACK),
+            in_=wc_raw[:].bitcast(U16).rearrange("p a (m t) -> p a m t", t=PACK),
+        )
+        nc.vector.tensor_copy(
+            out=wc_plane_perm[:].rearrange("p a (t m) -> p a m t", t=PACK),
+            in_=wc_plane[:].rearrange("p a (m t) -> p a m t", t=PACK),
+        )
+
+        cast_w(1, 0, False)
+        cast_w(1, 1, False)
+        quant(w_codes[1][:], w_plane[1][:], w_bf[1][:])
+
+        c_bf, c_codes, c_plane = {}, {}, {}
+
+        def cast_c(a, h, engine):
+            c_bf[a, h] = held([P, PACK * HALF], BF16, "c_bf%d%d" % (a, h))
+            dst = c_bf[a, h][:].rearrange("p (n e i) -> p n i e", e=4, i=PACK)
+            src = c_raw[a, h][:].rearrange("p i (n e) -> p n i e", e=4)
+            if engine == "vector":
+                nc.vector.tensor_copy(out=dst, in_=src)
+            else:
+                nc.scalar.copy(out=dst, in_=src)
+
+        def quant_c(a, h):
+            c_codes[a, h] = held([P, HALF], U32, "c_codes%d%d" % (a, h))
+            c_plane[a, h] = held([P, HALF], U8, "c_plane%d%d" % (a, h))
+            quant(c_codes[a, h][:], c_plane[a, h][:], c_bf[a, h][:])
+
+        pooled = {}
+
+        def neighbours(q):
+            banks = []
+            for g in range(LOOKS):
+                bank = psum.tile([P, PACK, CHUNK], F32, name="look_bank%d" % g, bufs=2)
+                for a in range(PASSES):
+                    for t in range(PACK):
+                        nc.tensor.matmul_mx(
+                            out=bank[:, t, :],
+                            lhsT=w_codes[a][:, P * t : P * (t + 1)].bitcast(FP8X4),
+                            lhsT_scale=w_plane[a][:, P * t : P * (t + 1)],
+                            rhs=look_words[g][:, a, 2 * CHUNK * q : 2 * CHUNK * (q + 1)].bitcast(FP4X4),
+                            rhs_scale=look_plane[:, a, J * g + CHUNK * q : J * g + CHUNK * (q + 1)],
+                            start=(a == 0 and t == 0),
+                            stop=(a == PASSES - 1 and t == PACK - 1),
+                        )
+                banks.append(bank)
+            first = ring.tile([P, CHUNK, PACK], F32, name="first")
+            nc.scalar.copy(out=first[:], in_=banks[0][:].rearrange("p t j -> p j t"))
+            pooled[q] = held([P, CHUNK, PACK], F32, "pooled%d" % q)
+            nc.vector.tensor_tensor(
+                out=pooled[q][:], in0=banks[1][:].rearrange("p t j -> p j t"), in1=first[:], op=ALU.max
+            )
+
+        summed, hidden, h_codes, h_plane = {}, {}, {}, {}
+
+        def add_own(q):
+            h, part = divmod(q, HALF // CHUNK)
+            cols = slice(CHUNK * part, CHUNK * (part + 1))
+            own = psum.tile([P, PACK, CHUNK], F32, name="own_bank", tag="late_bank", bufs=4)
+            for a in range(PASSES):
+                for t in range(PACK):
+                    nc.tensor.matmul_mx(
+                        out=own[:, t, :],
+                        lhsT=wc_perm[:, a, 2 * P * t : 2 * P * (t + 1)].bitcast(FP4X4),
+                        lhsT_scale=wc_plane_perm[:, a, P * t : P * (t + 1)],
+                        rhs=c_codes[a, h][:, cols].bitcast(FP8X4),
+                        rhs_scale=c_plane[a, h][:, cols],
+                        start=(a == 0 and t == 0),
+                        stop=(a == PASSES - 1 and t == PACK - 1),
+                    )
+            summed[q] = held([P, CHUNK, PACK], BF16, "summed%d" % q)
+            nc.vector.tensor_tensor(
+                out=summed[q][:], in0=own[:].rearrange("p t j -> p j t"), in1=pooled[q][:], op=ALU.add
+            )
+
+        def relu(q):
+            hidden[q] = held([P, CHUNK * PACK], BF16, "hidden%d" % q)
+            nc.vector.tensor_scalar_max(
+                out=hidden[q][:], in0=summed[q][:].rearrange("p j t -> p (j t)"), scalar1=0.0
+            )
+
+        def quant_h(q):
+            h_codes[q] = held([P, CHUNK], U32, "h_codes%d" % q)
+            h_plane[q] = held([P, CHUNK], U8, "h_plane%d" % q)
+            quant(h_codes[q][:], h_plane[q][:], hidden[q][:])
+
+        def project(q):
+            y_bank = psum.tile([P, N // P, CHUNK], F32, name="y_bank", tag="late_bank", bufs=4)
+            result = ring.tile([P, N // P, CHUNK], F32, name="result")
+            for s in range(N // P):
+                nc.tensor.matmul_mx(
+                    out=y_bank[:, s, :],
+                    lhsT=wd_raw[:, 2 * P * s : 2 * P * (s + 1)].bitcast(FP4X4),
+                    lhsT_scale=wd_plane[:, P * s : P * (s + 1)],
+                    rhs=h_codes[q][:].bitcast(FP8X4),
+                    rhs_scale=h_plane[q][:],
+                    start=True,
+                    stop=True,
+                )
+            for s in range(N // P):
+                nc.scalar.activation(
+                    out=result[:, s, :], in_=y_bank[:, s, :], func=ACT.Identity, bias=bias[:, s : s + 1]
+                )
+            nc.sync.dma_start(
+                out=out[:, CHUNK * q : CHUNK * (q + 1)].rearrange("(s p) j -> p s j", p=P), in_=result[:]
+            )
+
+        cast_c(0, 0, "scalar")
+        cast_c(1, 0, "vector")
+        quant_c(0, 0)
+        neighbours(0)
+        quant_c(1, 0)
+        neighbours(1)
+        cast_c(0, 1, "scalar")
+        add_own(0)
+        neighbours(2)
+        cast_c(1, 1, "scalar")
+        relu(0)
+        add_own(1)
+        quant_c(0, 1)
+        quant_h(0)
+        project(0)
+        relu(1)
+        neighbours(3)
+        quant_c(1, 1)
+        quant_h(1)
+        project(1)
+        add_own(2)
+        add_own(3)
+        relu(2)
+        relu(3)
+        quant_h(2)
+        quant_h(3)
+        project(2)
+        project(3)

@@ -44,10 +44,6 @@ def tile_list_pnet_bias_kernel(
         nc.sync.dma_start(
             out=tab_rows[0:32, :].bitcast(I32), in_=tab_scales.bitcast(I32).rearrange("a q t -> q a t")
         )
-        wc_raw = held([P, PASSES, 2 * R], U8, "wc_raw")
-        nc.sync.dma_start(
-            out=wc_raw[:].bitcast(I32), in_=wc_words.bitcast(I32).rearrange("a p n -> p a n")
-        )
         table = held([P, T], I32, "table")
         nc.sync.dma_start(
             out=table[:], in_=tab_words[0].rearrange("p t b -> p (t b)").bitcast(I32)
@@ -61,21 +57,23 @@ def tile_list_pnet_bias_kernel(
         nc.vector.memset(look_plane[:].rearrange("p a j -> p (a j)").bitcast(I32), 0)
         nc.gpsimd.memset(wd_plane[:].bitcast(I32), 0)
 
-        def load_rows(src, a, h, name):
-            raw = held([P, PACK, HALF], F32, name)
-            rows = src[512 * a : 512 * (a + 1), HALF * h : HALF * (h + 1)]
+        def load_rows(src, a, lo, hi, name):
+            raw = held([P, PACK, hi - lo], F32, name)
+            rows = src[512 * a : 512 * (a + 1), lo:hi]
             nc.sync.dma_start(out=raw[:], in_=rows.rearrange("(p i) n -> p i n", i=PACK))
             return raw
 
         w_raw = {}
-        w_raw[0, 0] = load_rows(w, 0, 0, "w_raw00")
         for q in range(4):
             nc.sync.dma_start(
                 out=wc_plane[32 * q : 32 * q + 4, :, :].bitcast(I32),
                 in_=wc_scales[:, 4 * q : 4 * q + 4, :].bitcast(I32).rearrange("a r n -> r a n"),
             )
-        w_raw[0, 1] = load_rows(w, 0, 1, "w_raw01")
-        w_raw[1, 0] = load_rows(w, 1, 0, "w_raw10")
+        w_raw[0] = load_rows(w, 0, 0, R, "w_raw0")
+        wc_raw = held([P, PASSES, 2 * R], U8, "wc_raw")
+        nc.sync.dma_start(
+            out=wc_raw[:].bitcast(I32), in_=wc_words.bitcast(I32).rearrange("a p n -> p a n")
+        )
 
         picked_rows = held([P, LOOKS * J], U8, "picked_rows")
         nc.vector.tensor_copy(out=picked_rows[:], in_=tab_rows[:].indirect(offsets[:]))
@@ -85,12 +83,11 @@ def tile_list_pnet_bias_kernel(
                 in_=picked_rows[8 * q : 8 * q + 8, :].bitcast(I32),
             )
 
-        w_raw[1, 1] = load_rows(w, 1, 1, "w_raw11")
-        c_raw = {}
-        c_raw[0, 0] = load_rows(c, 0, 0, "c_raw00")
-        c_raw[1, 0] = load_rows(c, 1, 0, "c_raw10")
-        c_raw[0, 1] = load_rows(c, 0, 1, "c_raw01")
-        c_raw[1, 1] = load_rows(c, 1, 1, "c_raw11")
+        w_raw[1] = load_rows(w, 1, 0, R, "w_raw1")
+        c_first = load_rows(c, 0, 0, J, "c_raw0")
+        c_raw = {(0, h): c_first[:, :, HALF * h : HALF * (h + 1)] for h in range(2)}
+        for h in range(2):
+            c_raw[1, h] = load_rows(c, 1, HALF * h, HALF * (h + 1), "c_raw1%d" % h)[:]
         wd_raw = held([P, 2 * N], U8, "wd_raw")
         nc.sync.dma_start(out=wd_raw[:].bitcast(I32), in_=wd_words[0].bitcast(I32))
         for q in range(4):
@@ -108,7 +105,7 @@ def tile_list_pnet_bias_kernel(
 
         def cast_w(a, h, on_vector):
             dst = w_bf[a][:].rearrange("p (t m i) -> p m i t", t=PACK, i=PACK)[:, 64 * h : 64 * (h + 1), :, :]
-            src = w_raw[a, h][:].rearrange("p i (m t) -> p m i t", t=PACK)
+            src = w_raw[a][:].rearrange("p i (m t) -> p m i t", t=PACK)[:, 64 * h : 64 * (h + 1), :, :]
             if on_vector:
                 nc.vector.tensor_copy(out=dst, in_=src)
             else:
@@ -136,18 +133,18 @@ def tile_list_pnet_bias_kernel(
         cast_w(0, 1, False)
         quant(w_codes[0][:], w_plane[0][:], w_bf[0][:])
         wc_perm = held([P, PASSES, 2 * R], U8, "wc_perm")
-        wc_plane_perm = held([P, PASSES, R], U8, "wc_plane_perm")
         nc.vector.tensor_copy(
             out=wc_perm[:].bitcast(U16).rearrange("p a (t m) -> p a m t", t=PACK),
             in_=wc_raw[:].bitcast(U16).rearrange("p a (m t) -> p a m t", t=PACK),
         )
+        wc_plane_perm = held([P, PASSES, R], U8, "w_bf0")
         nc.vector.tensor_copy(
             out=wc_plane_perm[:].rearrange("p a (t m) -> p a m t", t=PACK),
             in_=wc_plane[:].rearrange("p a (m t) -> p a m t", t=PACK),
         )
 
         cast_w(1, 0, False)
-        cast_w(1, 1, False)
+        cast_w(1, 1, True)
         quant(w_codes[1][:], w_plane[1][:], w_bf[1][:])
 
         c_bf, c_codes, c_plane = {}, {}, {}
@@ -155,7 +152,7 @@ def tile_list_pnet_bias_kernel(
         def cast_c(a, h, engine):
             c_bf[a, h] = held([P, PACK * HALF], BF16, "c_bf%d%d" % (a, h))
             dst = c_bf[a, h][:].rearrange("p (n e i) -> p n i e", e=4, i=PACK)
-            src = c_raw[a, h][:].rearrange("p i (n e) -> p n i e", e=4)
+            src = c_raw[a, h].rearrange("p i (n e) -> p n i e", e=4)
             if engine == "vector":
                 nc.vector.tensor_copy(out=dst, in_=src)
             else:
@@ -168,49 +165,74 @@ def tile_list_pnet_bias_kernel(
 
         pooled = {}
 
-        def neighbours(q):
-            banks = []
-            for g in range(LOOKS):
-                bank = psum.tile([P, PACK, CHUNK], F32, name="look_bank%d" % g, bufs=2)
-                for a in range(PASSES):
-                    for t in range(PACK):
-                        nc.tensor.matmul_mx(
-                            out=bank[:, t, :],
-                            lhsT=w_codes[a][:, P * t : P * (t + 1)].bitcast(FP8X4),
-                            lhsT_scale=w_plane[a][:, P * t : P * (t + 1)],
-                            rhs=look_words[g][:, a, 2 * CHUNK * q : 2 * CHUNK * (q + 1)].bitcast(FP4X4),
-                            rhs_scale=look_plane[:, a, J * g + CHUNK * q : J * g + CHUNK * (q + 1)],
-                            start=(a == 0 and t == 0),
-                            stop=(a == PASSES - 1 and t == PACK - 1),
-                        )
-                banks.append(bank)
-            first = ring.tile([P, CHUNK, PACK], F32, name="first")
-            nc.scalar.copy(out=first[:], in_=banks[0][:].rearrange("p t j -> p j t"))
-            pooled[q] = held([P, CHUNK, PACK], F32, "pooled%d" % q)
-            nc.vector.tensor_tensor(
-                out=pooled[q][:], in0=banks[1][:].rearrange("p t j -> p j t"), in1=first[:], op=ALU.max
-            )
+        def look_passes(g, q):
+            return [
+                (
+                    t,
+                    w_codes[a][:, P * t : P * (t + 1)].bitcast(FP8X4),
+                    w_plane[a][:, P * t : P * (t + 1)],
+                    look_words[g][:, a, 2 * CHUNK * q : 2 * CHUNK * (q + 1)].bitcast(FP4X4),
+                    look_plane[:, a, J * g + CHUNK * q : J * g + CHUNK * (q + 1)],
+                )
+                for a in range(PASSES)
+                for t in range(PACK)
+            ]
+
+        def own_passes(q):
+            h, part = divmod(q, HALF // CHUNK)
+            cols = slice(CHUNK * part, CHUNK * (part + 1))
+            return [
+                (
+                    t,
+                    wc_perm[:, a, 2 * P * t : 2 * P * (t + 1)].bitcast(FP4X4),
+                    wc_plane_perm[:, a, P * t : P * (t + 1)],
+                    c_codes[a, h][:, cols].bitcast(FP8X4),
+                    c_plane[a, h][:, cols],
+                )
+                for a in range(PASSES)
+                for t in range(PACK)
+            ]
+
+        def accumulate(bank, passes):
+            for n, (t, lhsT, lhsT_scale, rhs, rhs_scale) in enumerate(passes):
+                nc.tensor.matmul_mx(
+                    out=bank[:, t, :],
+                    lhsT=lhsT,
+                    lhsT_scale=lhsT_scale,
+                    rhs=rhs,
+                    rhs_scale=rhs_scale,
+                    start=(n == 0),
+                    stop=(n == len(passes) - 1),
+                )
+            return bank[:].rearrange("p t j -> p j t")
+
+        def look_bank(g):
+            return psum.tile([P, PACK, CHUNK], F32, name="look_bank%d" % g, bufs=2)
 
         summed, hidden, h_codes, h_plane = {}, {}, {}, {}
 
+        def neighbours(q):
+            sums = [accumulate(look_bank(g), look_passes(g, q)) for g in range(LOOKS)]
+            first = ring.tile([P, CHUNK, PACK], F32, name="first")
+            nc.scalar.copy(out=first[:], in_=sums[0])
+            pooled[q] = held([P, CHUNK, PACK], F32, "pooled%d" % q)
+            nc.vector.tensor_tensor(out=pooled[q][:], in0=sums[1], in1=first[:], op=ALU.max)
+
+        def joint(q):
+            sums = [accumulate(look_bank(g), look_passes(g, q) + own_passes(q)) for g in range(LOOKS)]
+            first = ring.tile([P, CHUNK, PACK], F32, name="first")
+            nc.scalar.activation(out=first[:], in_=sums[0], func=ACT.Relu)
+            hidden[q] = held([P, CHUNK * PACK], BF16, "hidden%d" % q)
+            nc.vector.tensor_tensor(
+                out=hidden[q][:].rearrange("p (j t) -> p j t", t=PACK), in0=sums[1], in1=first[:], op=ALU.max
+            )
+
         def add_own(q):
-            h, part = divmod(q, HALF // CHUNK)
-            cols = slice(CHUNK * part, CHUNK * (part + 1))
-            own = psum.tile([P, PACK, CHUNK], F32, name="own_bank", tag="late_bank", bufs=4)
-            for a in range(PASSES):
-                for t in range(PACK):
-                    nc.tensor.matmul_mx(
-                        out=own[:, t, :],
-                        lhsT=wc_perm[:, a, 2 * P * t : 2 * P * (t + 1)].bitcast(FP4X4),
-                        lhsT_scale=wc_plane_perm[:, a, P * t : P * (t + 1)],
-                        rhs=c_codes[a, h][:, cols].bitcast(FP8X4),
-                        rhs_scale=c_plane[a, h][:, cols],
-                        start=(a == 0 and t == 0),
-                        stop=(a == PASSES - 1 and t == PACK - 1),
-                    )
+            bank = psum.tile([P, PACK, CHUNK], F32, name="own_bank", tag="late_bank", bufs=4)
+            own = accumulate(bank, own_passes(q))
             summed[q] = held([P, CHUNK, PACK], BF16, "summed%d" % q)
             nc.vector.tensor_tensor(
-                out=summed[q][:], in0=own[:].rearrange("p t j -> p j t"), in1=pooled[q][:], op=ALU.add
+                out=summed[q][:], in0=own, in1=pooled[q][:], op=ALU.add
             )
 
         def relu(q):
@@ -246,29 +268,27 @@ def tile_list_pnet_bias_kernel(
             )
 
         cast_c(0, 0, "scalar")
-        cast_c(1, 0, "vector")
+        cast_c(0, 1, "scalar")
         quant_c(0, 0)
         neighbours(0)
-        quant_c(1, 0)
-        neighbours(1)
-        cast_c(0, 1, "scalar")
-        add_own(0)
-        neighbours(2)
-        cast_c(1, 1, "scalar")
-        relu(0)
-        add_own(1)
         quant_c(0, 1)
-        quant_h(0)
-        project(0)
-        relu(1)
-        neighbours(3)
+        neighbours(1)
+        cast_c(1, 0, "vector")
+        neighbours(2)
+        quant_c(1, 0)
+        cast_c(1, 1, "scalar")
+        add_own(0)
         quant_c(1, 1)
-        quant_h(1)
-        project(1)
+        add_own(1)
+        relu(0)
+        relu(1)
         add_own(2)
-        add_own(3)
+        quant_h(0)
+        quant_h(1)
+        joint(3)
         relu(2)
-        relu(3)
+        project(0)
+        project(1)
         quant_h(2)
         quant_h(3)
         project(2)

@@ -134,13 +134,13 @@ def tile_list_pnet_bias_kernel(
         quant(w_codes[0][:], w_plane[0][:], w_bf[0][:])
         wc_perm = held([P, PASSES, 2 * R], U8, "wc_perm")
         nc.vector.tensor_copy(
-            out=wc_perm[:].bitcast(U16).rearrange("p a (t m) -> p a m t", t=PACK),
-            in_=wc_raw[:].bitcast(U16).rearrange("p a (m t) -> p a m t", t=PACK),
+            out=wc_perm[:].bitcast(U16).rearrange("p a (t m) -> p a t m", t=PACK),
+            in_=wc_raw[:].bitcast(U16).rearrange("p a (m t) -> p a t m", t=PACK),
         )
         wc_plane_perm = held([P, PASSES, R], U8, "w_bf0")
         nc.vector.tensor_copy(
-            out=wc_plane_perm[:].rearrange("p a (t m) -> p a m t", t=PACK),
-            in_=wc_plane[:].rearrange("p a (m t) -> p a m t", t=PACK),
+            out=wc_plane_perm[:].rearrange("p a (t m) -> p a t m", t=PACK),
+            in_=wc_plane[:].rearrange("p a (m t) -> p a t m", t=PACK),
         )
 
         cast_w(1, 0, False)

@@ -22,7 +22,13 @@ PASSES = K // (P * PACK)
 LOOKS = 2
 CHUNK = 128
 CHUNKS = J // CHUNK
-HALF = 256
+LAST = CHUNKS - 1
+HALF = 2 * CHUNK
+ROWS = 32
+LOOK_AT, WC_AT, WD_AT, PLANE_W = 0, LOOKS * J, LOOKS * J + R, LOOKS * J + R + P
+
+W0_SCALAR = 48
+W1_SCALAR = 64
 
 
 def tile_list_pnet_bias_kernel(
@@ -31,70 +37,66 @@ def tile_list_pnet_bias_kernel(
     nc = tc.nc
     with ExitStack() as ctx:
         keep = ctx.enter_context(tc.tile_pool(name="keep", bufs=1))
-        ring = ctx.enter_context(tc.tile_pool(name="ring", bufs=4))
         psum = ctx.enter_context(tc.psum_pool(name="psum", bufs=1))
 
-        def held(shape, dtype, name):
-            return keep.tile(shape, dtype, name=name, align_bytes=64)
+        def held(shape, dtype, name, tag=None):
+            return keep.tile(shape, dtype, name=name, tag=tag or name, align_bytes=64)
 
         offsets = keep.tile([P, LOOKS * J // 16], U16, name="offsets")
         nc.sync.dma_start(offsets[:], offs)
 
         tab_rows = held([P, T], U8, "tab_rows")
+        wc_rows = held([P, R], U8, "wc_rows")
+        stage = held([P, PLANE_W], U8, "stage")
+        plane = held([P, PASSES, PLANE_W], U8, "plane")
         nc.sync.dma_start(
-            out=tab_rows[0:32, :].bitcast(I32), in_=tab_scales.bitcast(I32).rearrange("a q t -> q a t")
+            out=tab_rows[0:ROWS, :].bitcast(I32), in_=tab_scales.bitcast(I32).rearrange("a q t -> q a t")
         )
-        table = held([P, T], I32, "table")
         nc.sync.dma_start(
-            out=table[:], in_=tab_words[0].rearrange("p t b -> p (t b)").bitcast(I32)
+            out=wc_rows[0:ROWS, :].bitcast(I32), in_=wc_scales.bitcast(I32).rearrange("a q t -> q a t")
         )
-        wc_plane = held([P, PASSES, R], U8, "wc_plane")
-        wd_plane = held([P, N], U8, "wd_plane")
-        look_plane = held([P, PASSES, LOOKS * J], U8, "look_plane")
-        nc.gpsimd.memset(wc_plane[:].rearrange("p a r -> p (a r)").bitcast(I32), 0)
+        nc.sync.dma_start(
+            out=stage[0:ROWS, WD_AT:PLANE_W].bitcast(I32),
+            in_=wd_scales[0].bitcast(I32).rearrange("q (s n) -> (q s) n", s=2),
+        )
+        nc.gpsimd.memset(wc_rows[32:64, :].bitcast(I32), 0)
         nc.gpsimd.memset(tab_rows[32:64, :].bitcast(I32), 0)
+        nc.vector.memset(wc_rows[64:128, :].bitcast(I32), 0)
         nc.vector.memset(tab_rows[64:128, :].bitcast(I32), 0)
-        nc.vector.memset(look_plane[:].rearrange("p a j -> p (a j)").bitcast(I32), 0)
-        nc.gpsimd.memset(wd_plane[:].bitcast(I32), 0)
+        nc.vector.memset(plane[:].rearrange("p a j -> p (a j)").bitcast(I32), 0)
 
-        def load_rows(src, a, lo, hi, name):
-            raw = held([P, PACK, hi - lo], F32, name)
+        def load_rows(src, a, lo, hi, name, tag=None):
+            raw = held([P, PACK, hi - lo], F32, name, tag)
             rows = src[512 * a : 512 * (a + 1), lo:hi]
             nc.sync.dma_start(out=raw[:], in_=rows.rearrange("(p i) n -> p i n", i=PACK))
             return raw
 
-        w_raw = {}
-        for q in range(4):
-            nc.sync.dma_start(
-                out=wc_plane[32 * q : 32 * q + 4, :, :].bitcast(I32),
-                in_=wc_scales[:, 4 * q : 4 * q + 4, :].bitcast(I32).rearrange("a r n -> r a n"),
-            )
-        w_raw[0] = load_rows(w, 0, 0, R, "w_raw0")
-        wc_raw = held([P, PASSES, 2 * R], U8, "wc_raw")
-        nc.sync.dma_start(
-            out=wc_raw[:].bitcast(I32), in_=wc_words.bitcast(I32).rearrange("a p n -> p a n")
-        )
+        w_raw = {0: load_rows(w, 0, 0, R, "w_raw0")}
+        table = held([P, T], I32, "table")
+        nc.sync.dma_start(out=table[:], in_=tab_words[0].rearrange("p t b -> p (t b)").bitcast(I32))
 
         picked_rows = held([P, LOOKS * J], U8, "picked_rows")
         nc.vector.tensor_copy(out=picked_rows[:], in_=tab_rows[:].indirect(offsets[:]))
+        nc.vector.tensor_copy(
+            out=stage[:, WC_AT:WD_AT].rearrange("p (t m) -> p t m", t=PACK),
+            in_=wc_rows[:].rearrange("p (m t) -> p t m", t=PACK),
+        )
+        nc.vector.tensor_copy(
+            out=stage[0:ROWS, LOOK_AT:WC_AT].bitcast(I32), in_=picked_rows[0:ROWS, :].bitcast(I32)
+        )
         for q in range(4):
             nc.sync.dma_start(
-                out=look_plane[32 * q : 32 * q + 4, :, :].bitcast(I32),
-                in_=picked_rows[8 * q : 8 * q + 8, :].bitcast(I32),
+                out=plane[32 * q : 32 * q + 4, :, :].bitcast(I32),
+                in_=stage[8 * q : 8 * q + 8, :].bitcast(I32),
             )
 
         w_raw[1] = load_rows(w, 1, 0, R, "w_raw1")
+        wc_raw = held([P, PASSES, 2 * R], U8, "wc_raw")
+        nc.sync.dma_start(out=wc_raw[:].bitcast(I32), in_=wc_words.bitcast(I32).rearrange("a p n -> p a n"))
         c_first = load_rows(c, 0, 0, J, "c_raw0")
-        c_raw = {(0, h): c_first[:, :, HALF * h : HALF * (h + 1)] for h in range(2)}
-        for h in range(2):
-            c_raw[1, h] = load_rows(c, 1, HALF * h, HALF * (h + 1), "c_raw1%d" % h)[:]
+        c_second = [load_rows(c, 1, HALF * h, HALF * (h + 1), "c_raw1%d" % h) for h in range(2)]
         wd_raw = held([P, 2 * N], U8, "wd_raw")
         nc.sync.dma_start(out=wd_raw[:].bitcast(I32), in_=wd_words[0].bitcast(I32))
-        for q in range(4):
-            nc.sync.dma_start(
-                out=wd_plane[32 * q : 32 * q + 4, :].bitcast(I32),
-                in_=wd_scales[0, 4 * q : 4 * q + 4, :].bitcast(I32),
-            )
         bias = held([P, N // P], F32, "bias")
         with nc.allow_non_contiguous_dma(reason="one bias value a partition"):
             nc.sync.dma_start(out=bias[:], in_=b.rearrange("(s p) -> p s", p=P))
@@ -103,137 +105,151 @@ def tile_list_pnet_bias_kernel(
         w_codes = [held([P, R], U32, "w_codes%d" % a) for a in range(PASSES)]
         w_plane = [held([P, R], U8, "w_plane%d" % a) for a in range(PASSES)]
 
-        def cast_w(a, h, on_vector):
-            dst = w_bf[a][:].rearrange("p (t m i) -> p m i t", t=PACK, i=PACK)[:, 64 * h : 64 * (h + 1), :, :]
-            src = w_raw[a][:].rearrange("p i (m t) -> p m i t", t=PACK)[:, 64 * h : 64 * (h + 1), :, :]
+        def round_copy(on_vector, dst, src):
             if on_vector:
                 nc.vector.tensor_copy(out=dst, in_=src)
             else:
                 nc.scalar.copy(out=dst, in_=src)
 
-        def quant(codes, plane, src):
-            nc.vector.quantize_mx(out=codes.bitcast(FP8X4), scales=plane, in_=src)
+        def cast_w(a, lo, hi, on_vector):
+            dst = w_bf[a][:].rearrange("p (t m i) -> p m i t", t=PACK, i=PACK)[:, lo:hi, :, :]
+            src = w_raw[a][:].rearrange("p i (m t) -> p m i t", t=PACK)[:, lo:hi, :, :]
+            round_copy(on_vector, dst, src)
 
-        cast_w(0, 0, False)
+        def quant(codes, scales, src):
+            nc.vector.quantize_mx(out=codes.bitcast(FP8X4), scales=scales, in_=src)
 
-        look_words = []
-        for g in range(LOOKS):
-            picked = held([P, J], U32, "picked%d" % g)
+        picked, look_words = {}, {}
+
+        def pick_words(g, h):
+            picked[g, h] = held([P, HALF], U32, "picked%d%d" % (g, h))
+            at = (g * J + h * HALF) // 16
             nc.vector.tensor_copy(
-                out=picked[:],
-                in_=table[:].bitcast(U32).indirect(offsets[:, g * J // 16 : (g + 1) * J // 16]),
+                out=picked[g, h][:], in_=table[:].bitcast(U32).indirect(offsets[:, at : at + HALF // 16])
             )
-            parted = held([P, PASSES, 2 * J], U8, "parted%d" % g)
-            nc.vector.tensor_copy(
-                out=parted[:].bitcast(U16),
-                in_=picked[:].bitcast(U16).rearrange("p (j d) -> p d j", d=PASSES),
-            )
-            look_words.append(parted)
 
-        cast_w(0, 1, False)
+        def part_words(g, h):
+            look_words[g, h] = held([P, PASSES, 2 * HALF], U8, "parted%d%d" % (g, h))
+            nc.vector.tensor_copy(
+                out=look_words[g, h][:].bitcast(U16),
+                in_=picked[g, h][:].bitcast(U16).rearrange("p (j d) -> p d j", d=PASSES),
+            )
+
+        cast_w(0, 0, W0_SCALAR, False)
+        cast_w(0, W0_SCALAR, P, True)
         quant(w_codes[0][:], w_plane[0][:], w_bf[0][:])
+        pick_words(0, 0)
+        pick_words(0, 1)
+        part_words(0, 0)
+        pick_words(1, 0)
+        part_words(0, 1)
+        pick_words(1, 1)
+        part_words(1, 0)
+        cast_w(1, 0, W1_SCALAR, False)
+        cast_w(1, W1_SCALAR, P, True)
+        part_words(1, 1)
+        quant(w_codes[1][:], w_plane[1][:], w_bf[1][:])
         wc_perm = held([P, PASSES, 2 * R], U8, "wc_perm")
         nc.vector.tensor_copy(
             out=wc_perm[:].bitcast(U16).rearrange("p a (t m) -> p a t m", t=PACK),
             in_=wc_raw[:].bitcast(U16).rearrange("p a (m t) -> p a t m", t=PACK),
         )
-        wc_plane_perm = held([P, PASSES, R], U8, "w_bf0")
-        nc.vector.tensor_copy(
-            out=wc_plane_perm[:].rearrange("p a (t m) -> p a t m", t=PACK),
-            in_=wc_plane[:].rearrange("p a (m t) -> p a t m", t=PACK),
-        )
-
-        cast_w(1, 0, False)
-        cast_w(1, 1, True)
-        quant(w_codes[1][:], w_plane[1][:], w_bf[1][:])
 
         c_bf, c_codes, c_plane = {}, {}, {}
 
-        def cast_c(a, h, engine):
-            c_bf[a, h] = held([P, PACK * HALF], BF16, "c_bf%d%d" % (a, h))
-            dst = c_bf[a, h][:].rearrange("p (n e i) -> p n i e", e=4, i=PACK)
-            src = c_raw[a, h].rearrange("p i (n e) -> p n i e", e=4)
-            if engine == "vector":
-                nc.vector.tensor_copy(out=dst, in_=src)
-            else:
-                nc.scalar.copy(out=dst, in_=src)
+        def cast_c(a, q, width, raw, lo, on_vector):
+            c_bf[a, q] = held([P, PACK * width], BF16, "c_bf%d%d" % (a, q))
+            dst = c_bf[a, q][:].rearrange("p (n e i) -> p n i e", e=4, i=PACK)
+            src = raw[:, :, lo : lo + width].rearrange("p i (n e) -> p n i e", e=4)
+            round_copy(on_vector, dst, src)
 
-        def quant_c(a, h):
-            c_codes[a, h] = held([P, HALF], U32, "c_codes%d%d" % (a, h))
-            c_plane[a, h] = held([P, HALF], U8, "c_plane%d%d" % (a, h))
-            quant(c_codes[a, h][:], c_plane[a, h][:], c_bf[a, h][:])
+        def quant_c(a, q):
+            width = c_bf[a, q].shape[1] // PACK
+            codes = held([P, width], U32, "c_codes%d%d" % (a, q))
+            scales = held([P, width], U8, "c_plane%d%d" % (a, q))
+            quant(codes[:], scales[:], c_bf[a, q][:])
+            for part in range(width // CHUNK):
+                cols = slice(CHUNK * part, CHUNK * (part + 1))
+                c_codes[a, q + part] = codes[:, cols]
+                c_plane[a, q + part] = scales[:, cols]
 
-        pooled = {}
-
-        def look_passes(g, q):
-            return [
-                (
-                    t,
-                    w_codes[a][:, P * t : P * (t + 1)].bitcast(FP8X4),
-                    w_plane[a][:, P * t : P * (t + 1)],
-                    look_words[g][:, a, 2 * CHUNK * q : 2 * CHUNK * (q + 1)].bitcast(FP4X4),
-                    look_plane[:, a, J * g + CHUNK * q : J * g + CHUNK * (q + 1)],
-                )
-                for a in range(PASSES)
-                for t in range(PACK)
-            ]
-
-        def own_passes(q):
-            h, part = divmod(q, HALF // CHUNK)
-            cols = slice(CHUNK * part, CHUNK * (part + 1))
-            return [
-                (
-                    t,
-                    wc_perm[:, a, 2 * P * t : 2 * P * (t + 1)].bitcast(FP4X4),
-                    wc_plane_perm[:, a, P * t : P * (t + 1)],
-                    c_codes[a, h][:, cols].bitcast(FP8X4),
-                    c_plane[a, h][:, cols],
-                )
-                for a in range(PASSES)
-                for t in range(PACK)
-            ]
-
-        def accumulate(bank, passes):
-            for n, (t, lhsT, lhsT_scale, rhs, rhs_scale) in enumerate(passes):
+        def passes(bank, operands, start, stop):
+            for t in range(PACK):
+                lhsT, lhsT_scale, rhs, rhs_scale = operands(t)
                 nc.tensor.matmul_mx(
                     out=bank[:, t, :],
                     lhsT=lhsT,
                     lhsT_scale=lhsT_scale,
                     rhs=rhs,
                     rhs_scale=rhs_scale,
-                    start=(n == 0),
-                    stop=(n == len(passes) - 1),
+                    start=(start and t == 0),
+                    stop=(stop and t == PACK - 1),
                 )
+
+        def look_operands(g, q, a):
+            at = LOOK_AT + J * g + CHUNK * q
+            return lambda t: (
+                w_codes[a][:, P * t : P * (t + 1)].bitcast(FP8X4),
+                w_plane[a][:, P * t : P * (t + 1)],
+                look_words[g, q // 2][:, a, 2 * CHUNK * (q % 2) : 2 * CHUNK * (q % 2 + 1)].bitcast(FP4X4),
+                plane[:, a, at : at + CHUNK],
+            )
+
+        def own_operands(q, a):
+            return lambda t: (
+                wc_perm[:, a, 2 * P * t : 2 * P * (t + 1)].bitcast(FP4X4),
+                plane[:, a, WC_AT + P * t : WC_AT + P * (t + 1)],
+                c_codes[a, q].bitcast(FP8X4),
+                c_plane[a, q],
+            )
+
+        def bank_tile(shape, name, g, q):
+            return psum.tile(shape, F32, name=name, tag="bank%d%d" % (g, q))
+
+        def woven(bank):
             return bank[:].rearrange("p t j -> p j t")
 
-        def look_bank(g):
-            return psum.tile([P, PACK, CHUNK], F32, name="look_bank%d" % g, bufs=2)
+        look_bank = {}
+        for g in range(LOOKS):
+            for q in range(CHUNKS):
+                look_bank[g, q] = bank_tile([P, PACK, CHUNK], "look_bank", g, q)
+        for g in range(LOOKS):
+            for q in range(CHUNKS):
+                passes(look_bank[g, q], look_operands(g, q, 0), True, False)
+        for q in range(CHUNKS):
+            for g in range(LOOKS):
+                passes(look_bank[g, q], look_operands(g, q, 1), False, q != LAST)
 
-        summed, hidden, h_codes, h_plane = {}, {}, {}, {}
+        first, pooled, own_bank, summed, hidden, h_codes, h_plane = {}, {}, {}, {}, {}, {}, {}
 
-        def neighbours(q):
-            sums = [accumulate(look_bank(g), look_passes(g, q)) for g in range(LOOKS)]
-            first = ring.tile([P, CHUNK, PACK], F32, name="first")
-            nc.scalar.copy(out=first[:], in_=sums[0])
-            pooled[q] = held([P, CHUNK, PACK], F32, "pooled%d" % q)
-            nc.vector.tensor_tensor(out=pooled[q][:], in0=sums[1], in1=first[:], op=ALU.max)
+        def copy_first(q):
+            first[q] = held([P, CHUNK, PACK], F32, "first%d" % q)
+            if q == LAST:
+                nc.scalar.activation(out=first[q][:], in_=woven(look_bank[0, q]), func=ACT.Relu)
+            else:
+                nc.scalar.copy(out=first[q][:], in_=woven(look_bank[0, q]))
 
-        def joint(q):
-            sums = [accumulate(look_bank(g), look_passes(g, q) + own_passes(q)) for g in range(LOOKS)]
-            first = ring.tile([P, CHUNK, PACK], F32, name="first")
-            nc.scalar.activation(out=first[:], in_=sums[0], func=ACT.Relu)
-            hidden[q] = held([P, CHUNK * PACK], BF16, "hidden%d" % q)
-            nc.vector.tensor_tensor(
-                out=hidden[q][:].rearrange("p (j t) -> p j t", t=PACK), in0=sums[1], in1=first[:], op=ALU.max
-            )
+        def pool_pair(q):
+            if q == LAST:
+                hidden[q] = held([P, CHUNK * PACK], BF16, "hidden%d" % q)
+                dst = hidden[q][:].rearrange("p (j t) -> p j t", t=PACK)
+            else:
+                pooled[q] = held([P, CHUNK, PACK], F32, "pooled%d" % q)
+                dst = pooled[q][:]
+            nc.vector.tensor_tensor(out=dst, in0=woven(look_bank[1, q]), in1=first[q][:], op=ALU.max)
+
+        def own(q, a):
+            if q == LAST:
+                for g in range(LOOKS):
+                    passes(look_bank[g, q], own_operands(q, a), False, a == PASSES - 1)
+                return
+            if a == 0:
+                own_bank[q] = bank_tile([P, PACK, CHUNK], "own_bank", 0, q)
+            passes(own_bank[q], own_operands(q, a), a == 0, a == PASSES - 1)
 
         def add_own(q):
-            bank = psum.tile([P, PACK, CHUNK], F32, name="own_bank", tag="late_bank", bufs=4)
-            own = accumulate(bank, own_passes(q))
             summed[q] = held([P, CHUNK, PACK], BF16, "summed%d" % q)
-            nc.vector.tensor_tensor(
-                out=summed[q][:], in0=own, in1=pooled[q][:], op=ALU.add
-            )
+            nc.vector.tensor_tensor(out=summed[q][:], in0=woven(own_bank[q]), in1=pooled[q][:], op=ALU.add)
 
         def relu(q):
             hidden[q] = held([P, CHUNK * PACK], BF16, "hidden%d" % q)
@@ -247,13 +263,13 @@ def tile_list_pnet_bias_kernel(
             quant(h_codes[q][:], h_plane[q][:], hidden[q][:])
 
         def project(q):
-            y_bank = psum.tile([P, N // P, CHUNK], F32, name="y_bank", tag="late_bank", bufs=4)
-            result = ring.tile([P, N // P, CHUNK], F32, name="result")
+            y_bank = bank_tile([P, N // P, CHUNK], "y_bank", 0 if q == LAST else 1, q)
+            result = held([P, N // P, CHUNK], F32, "result%d" % q)
             for s in range(N // P):
                 nc.tensor.matmul_mx(
                     out=y_bank[:, s, :],
                     lhsT=wd_raw[:, 2 * P * s : 2 * P * (s + 1)].bitcast(FP4X4),
-                    lhsT_scale=wd_plane[:, P * s : P * (s + 1)],
+                    lhsT_scale=plane[:, s, WD_AT:PLANE_W],
                     rhs=h_codes[q][:].bitcast(FP8X4),
                     rhs_scale=h_plane[q][:],
                     start=True,
@@ -267,28 +283,44 @@ def tile_list_pnet_bias_kernel(
                 out=out[:, CHUNK * q : CHUNK * (q + 1)].rearrange("(s p) j -> p s j", p=P), in_=result[:]
             )
 
-        cast_c(0, 0, "scalar")
-        cast_c(0, 1, "scalar")
+        copy_first(0)
+        cast_c(0, 0, 256, c_first, 0, True)
+        cast_c(0, 2, 256, c_first, 256, True)
+        copy_first(1)
         quant_c(0, 0)
-        neighbours(0)
-        quant_c(0, 1)
-        neighbours(1)
-        cast_c(1, 0, "vector")
-        neighbours(2)
+        pool_pair(0)
+        quant_c(0, 2)
+        copy_first(2)
+        pool_pair(1)
+        own(0, 0)
+        own(1, 0)
+        cast_c(1, 0, 128, c_second[0], 0, False)
         quant_c(1, 0)
-        cast_c(1, 1, "scalar")
-        add_own(0)
+        pool_pair(2)
+        own(2, 0)
+        own(0, 1)
+        cast_c(1, 1, 128, c_second[0], 128, False)
         quant_c(1, 1)
+        own(3, 0)
+        own(1, 1)
+        add_own(0)
+        cast_c(1, 2, 128, c_second[1], 0, False)
+        cast_c(1, 3, 128, c_second[1], 128, False)
+        quant_c(1, 2)
+        quant_c(1, 3)
+        own(2, 1)
+        own(3, 1)
         add_own(1)
         relu(0)
-        relu(1)
         add_own(2)
+        copy_first(3)
+        relu(1)
         quant_h(0)
         quant_h(1)
-        joint(3)
-        relu(2)
         project(0)
         project(1)
+        relu(2)
+        pool_pair(3)
         quant_h(2)
         quant_h(3)
         project(2)

@@ -28,7 +28,7 @@ ROWS = 32
 LOOK_AT, WC_AT, WD_AT, PLANE_W = 0, LOOKS * J, LOOKS * J + R, LOOKS * J + R + P
 
 W0_SCALAR = 48
-W1_SCALAR = 64
+W1_SCALAR = 96
 
 
 def tile_list_pnet_bias_kernel(
@@ -72,6 +72,9 @@ def tile_list_pnet_bias_kernel(
             return raw
 
         w_raw = {0: load_rows(w, 0, 0, R, "w_raw0")}
+        bias = held([P, N // P], F32, "bias")
+        with nc.allow_non_contiguous_dma(reason="one bias value a partition"):
+            nc.sync.dma_start(out=bias[:], in_=b.rearrange("(s p) -> p s", p=P))
         table = held([P, T], I32, "table")
         nc.sync.dma_start(out=table[:], in_=tab_words[0].rearrange("p t b -> p (t b)").bitcast(I32))
 
@@ -91,30 +94,31 @@ def tile_list_pnet_bias_kernel(
             )
 
         w_raw[1] = load_rows(w, 1, 0, R, "w_raw1")
+        c_raw = {}
         wc_raw = held([P, PASSES, 2 * R], U8, "wc_raw")
         nc.sync.dma_start(out=wc_raw[:].bitcast(I32), in_=wc_words.bitcast(I32).rearrange("a p n -> p a n"))
-        c_first = load_rows(c, 0, 0, J, "c_raw0")
-        c_second = [load_rows(c, 1, HALF * h, HALF * (h + 1), "c_raw1%d" % h) for h in range(2)]
+        c_raw[0] = load_rows(c, 0, 0, J, "c_raw0")
+        c_raw[1, 0] = load_rows(c, 1, 0, HALF, "c_raw1a")
+        c_raw[1, 1] = load_rows(c, 1, HALF, J, "c_raw1b")
         wd_raw = held([P, 2 * N], U8, "wd_raw")
         nc.sync.dma_start(out=wd_raw[:].bitcast(I32), in_=wd_words[0].bitcast(I32))
-        bias = held([P, N // P], F32, "bias")
-        with nc.allow_non_contiguous_dma(reason="one bias value a partition"):
-            nc.sync.dma_start(out=bias[:], in_=b.rearrange("(s p) -> p s", p=P))
 
         w_bf = [held([P, PACK * R], BF16, "w_bf%d" % a) for a in range(PASSES)]
         w_codes = [held([P, R], U32, "w_codes%d" % a) for a in range(PASSES)]
         w_plane = [held([P, R], U8, "w_plane%d" % a) for a in range(PASSES)]
 
-        def round_copy(on_vector, dst, src):
-            if on_vector:
+        def round_copy(engine, dst, src):
+            if engine == "vector":
                 nc.vector.tensor_copy(out=dst, in_=src)
-            else:
+            elif engine == "scalar":
                 nc.scalar.copy(out=dst, in_=src)
+            else:
+                nc.gpsimd.tensor_scalar(out=dst, in0=src, scalar1=1.0, scalar2=0.0, op0=ALU.mult, op1=ALU.add)
 
-        def cast_w(a, lo, hi, on_vector):
+        def cast_w(a, lo, hi, engine):
             dst = w_bf[a][:].rearrange("p (t m i) -> p m i t", t=PACK, i=PACK)[:, lo:hi, :, :]
             src = w_raw[a][:].rearrange("p i (m t) -> p m i t", t=PACK)[:, lo:hi, :, :]
-            round_copy(on_vector, dst, src)
+            round_copy(engine, dst, src)
 
         def quant(codes, scales, src):
             nc.vector.quantize_mx(out=codes.bitcast(FP8X4), scales=scales, in_=src)
@@ -122,7 +126,7 @@ def tile_list_pnet_bias_kernel(
         picked, look_words = {}, {}
 
         def pick_words(g, h):
-            picked[g, h] = held([P, HALF], U32, "picked%d%d" % (g, h))
+            picked[g, h] = held([P, HALF], U32, "picked%d%d" % (g, h), "picked%d" % h)
             at = (g * J + h * HALF) // 16
             nc.vector.tensor_copy(
                 out=picked[g, h][:], in_=table[:].bitcast(U32).indirect(offsets[:, at : at + HALF // 16])
@@ -135,8 +139,8 @@ def tile_list_pnet_bias_kernel(
                 in_=picked[g, h][:].bitcast(U16).rearrange("p (j d) -> p d j", d=PASSES),
             )
 
-        cast_w(0, 0, W0_SCALAR, False)
-        cast_w(0, W0_SCALAR, P, True)
+        cast_w(0, 0, W0_SCALAR, "scalar")
+        cast_w(0, W0_SCALAR, P, "vector")
         quant(w_codes[0][:], w_plane[0][:], w_bf[0][:])
         pick_words(0, 0)
         pick_words(0, 1)
@@ -145,23 +149,29 @@ def tile_list_pnet_bias_kernel(
         part_words(0, 1)
         pick_words(1, 1)
         part_words(1, 0)
-        cast_w(1, 0, W1_SCALAR, False)
-        cast_w(1, W1_SCALAR, P, True)
+        cast_w(1, 0, W1_SCALAR, "scalar")
+        cast_w(1, W1_SCALAR, P, "vector")
         part_words(1, 1)
         quant(w_codes[1][:], w_plane[1][:], w_bf[1][:])
         wc_perm = held([P, PASSES, 2 * R], U8, "wc_perm")
-        nc.vector.tensor_copy(
-            out=wc_perm[:].bitcast(U16).rearrange("p a (t m) -> p a t m", t=PACK),
-            in_=wc_raw[:].bitcast(U16).rearrange("p a (m t) -> p a t m", t=PACK),
-        )
+
+        def deal_wc():
+            nc.vector.tensor_copy(
+                out=wc_perm[:].bitcast(U16).rearrange("p a (t m) -> p a t m", t=PACK),
+                in_=wc_raw[:].bitcast(U16).rearrange("p a (m t) -> p a t m", t=PACK),
+            )
 
         c_bf, c_codes, c_plane = {}, {}, {}
 
-        def cast_c(a, q, width, raw, lo, on_vector):
+        def cast_c(a, q, width, raw, lo, engine):
             c_bf[a, q] = held([P, PACK * width], BF16, "c_bf%d%d" % (a, q))
-            dst = c_bf[a, q][:].rearrange("p (n e i) -> p n i e", e=4, i=PACK)
-            src = raw[:, :, lo : lo + width].rearrange("p i (n e) -> p n i e", e=4)
-            round_copy(on_vector, dst, src)
+            if engine == "gpsimd":
+                dst = c_bf[a, q][:].rearrange("p (n i) -> p n i", i=PACK)
+                src = raw[:, :, lo : lo + width].rearrange("p i n -> p n i")
+            else:
+                dst = c_bf[a, q][:].rearrange("p (n e i) -> p n i e", e=4, i=PACK)
+                src = raw[:, :, lo : lo + width].rearrange("p i (n e) -> p n i e", e=4)
+            round_copy(engine, dst, src)
 
         def quant_c(a, q):
             width = c_bf[a, q].shape[1] // PACK
@@ -239,13 +249,12 @@ def tile_list_pnet_bias_kernel(
             nc.vector.tensor_tensor(out=dst, in0=woven(look_bank[1, q]), in1=first[q][:], op=ALU.max)
 
         def own(q, a):
-            if q == LAST:
-                for g in range(LOOKS):
-                    passes(look_bank[g, q], own_operands(q, a), False, a == PASSES - 1)
-                return
             if a == 0:
                 own_bank[q] = bank_tile([P, PACK, CHUNK], "own_bank", 0, q)
             passes(own_bank[q], own_operands(q, a), a == 0, a == PASSES - 1)
+
+        def own_joint(g, a):
+            passes(look_bank[g, LAST], own_operands(LAST, a), False, a == PASSES - 1)
 
         def add_own(q):
             summed[q] = held([P, CHUNK, PACK], BF16, "summed%d" % q)
@@ -283,9 +292,10 @@ def tile_list_pnet_bias_kernel(
                 out=out[:, CHUNK * q : CHUNK * (q + 1)].rearrange("(s p) j -> p s j", p=P), in_=result[:]
             )
 
+        deal_wc()
         copy_first(0)
-        cast_c(0, 0, 256, c_first, 0, True)
-        cast_c(0, 2, 256, c_first, 256, True)
+        cast_c(0, 0, 256, c_raw[0], 0, "vector")
+        cast_c(0, 2, 256, c_raw[0], 256, "vector")
         copy_first(1)
         quant_c(0, 0)
         pool_pair(0)
@@ -294,22 +304,24 @@ def tile_list_pnet_bias_kernel(
         pool_pair(1)
         own(0, 0)
         own(1, 0)
-        cast_c(1, 0, 128, c_second[0], 0, False)
+        cast_c(1, 0, 128, c_raw[1, 0], 0, "scalar")
         quant_c(1, 0)
         pool_pair(2)
         own(2, 0)
         own(0, 1)
-        cast_c(1, 1, 128, c_second[0], 128, False)
+        cast_c(1, 1, 128, c_raw[1, 0], 128, "scalar")
         quant_c(1, 1)
-        own(3, 0)
+        own_joint(0, 0)
+        own_joint(1, 0)
         own(1, 1)
         add_own(0)
-        cast_c(1, 2, 128, c_second[1], 0, False)
-        cast_c(1, 3, 128, c_second[1], 128, False)
+        cast_c(1, 2, 128, c_raw[1, 1], 0, "scalar")
+        cast_c(1, 3, 128, c_raw[1, 1], 128, "scalar")
         quant_c(1, 2)
         quant_c(1, 3)
         own(2, 1)
-        own(3, 1)
+        own_joint(0, 1)
+        own_joint(1, 1)
         add_own(1)
         relu(0)
         add_own(2)

@@ -25,10 +25,10 @@ CHUNKS = J // CHUNK
 LAST = CHUNKS - 1
 HALF = 2 * CHUNK
 ROWS = 32
-LOOK_AT, WC_AT, WD_AT, PLANE_W = 0, LOOKS * J, LOOKS * J + R, LOOKS * J + R + P
+LOOK_AT, WC_AT, PLANE_W = 0, LOOKS * J, LOOKS * J + R
 
 W0_SCALAR = 48
-W1_SCALAR = 96
+W1_SCALAR = 80
 
 
 def tile_list_pnet_bias_kernel(
@@ -55,10 +55,6 @@ def tile_list_pnet_bias_kernel(
         nc.sync.dma_start(
             out=wc_rows[0:ROWS, :].bitcast(I32), in_=wc_scales.bitcast(I32).rearrange("a q t -> q a t")
         )
-        nc.sync.dma_start(
-            out=stage[0:ROWS, WD_AT:PLANE_W].bitcast(I32),
-            in_=wd_scales[0].bitcast(I32).rearrange("q (s n) -> (q s) n", s=2),
-        )
         nc.gpsimd.memset(wc_rows[32:64, :].bitcast(I32), 0)
         nc.gpsimd.memset(tab_rows[32:64, :].bitcast(I32), 0)
         nc.vector.memset(wc_rows[64:128, :].bitcast(I32), 0)
@@ -81,7 +77,7 @@ def tile_list_pnet_bias_kernel(
         picked_rows = held([P, LOOKS * J], U8, "picked_rows")
         nc.vector.tensor_copy(out=picked_rows[:], in_=tab_rows[:].indirect(offsets[:]))
         nc.vector.tensor_copy(
-            out=stage[:, WC_AT:WD_AT].rearrange("p (t m) -> p t m", t=PACK),
+            out=stage[:, WC_AT:PLANE_W].rearrange("p (t m) -> p t m", t=PACK),
             in_=wc_rows[:].rearrange("p (m t) -> p t m", t=PACK),
         )
         nc.vector.tensor_copy(
@@ -102,6 +98,13 @@ def tile_list_pnet_bias_kernel(
         c_raw[1, 1] = load_rows(c, 1, HALF, J, "c_raw1b")
         wd_raw = held([P, 2 * N], U8, "wd_raw")
         nc.sync.dma_start(out=wd_raw[:].bitcast(I32), in_=wd_words[0].bitcast(I32))
+        wd_plane = held([P, N], U8, "wd_plane")
+        nc.gpsimd.memset(wd_plane[:].bitcast(I32), 0)
+        for q in range(4):
+            nc.sync.dma_start(
+                out=wd_plane[32 * q : 32 * q + 4, :].bitcast(I32),
+                in_=wd_scales[0, 4 * q : 4 * q + 4, :].bitcast(I32),
+            )
 
         w_bf = [held([P, PACK * R], BF16, "w_bf%d" % a) for a in range(PASSES)]
         w_codes = [held([P, R], U32, "w_codes%d" % a) for a in range(PASSES)]
@@ -262,9 +265,11 @@ def tile_list_pnet_bias_kernel(
 
         def relu(q):
             hidden[q] = held([P, CHUNK * PACK], BF16, "hidden%d" % q)
-            nc.vector.tensor_scalar_max(
-                out=hidden[q][:], in0=summed[q][:].rearrange("p j t -> p (j t)"), scalar1=0.0
-            )
+            flat = summed[q][:].rearrange("p j t -> p (j t)")
+            if q in (0,):
+                nc.scalar.activation(out=hidden[q][:], in_=flat, func=ACT.Relu)
+            else:
+                nc.vector.tensor_scalar_max(out=hidden[q][:], in0=flat, scalar1=0.0)
 
         def quant_h(q):
             h_codes[q] = held([P, CHUNK], U32, "h_codes%d" % q)
@@ -278,7 +283,7 @@ def tile_list_pnet_bias_kernel(
                 nc.tensor.matmul_mx(
                     out=y_bank[:, s, :],
                     lhsT=wd_raw[:, 2 * P * s : 2 * P * (s + 1)].bitcast(FP4X4),
-                    lhsT_scale=plane[:, s, WD_AT:PLANE_W],
+                    lhsT_scale=wd_plane[:, P * s : P * (s + 1)],
                     rhs=h_codes[q][:].bitcast(FP8X4),
                     rhs_scale=h_plane[q][:],
                     start=True,

@@ -27,7 +27,7 @@ HALF = 2 * CHUNK
 ROWS = 32
 LOOK_AT, WC_AT, PLANE_W = 0, LOOKS * J, LOOKS * J + R
 
-W0_SCALAR = 48
+W0_SCALAR = 64
 W1_SCALAR = 80
 
 
@@ -128,33 +128,33 @@ def tile_list_pnet_bias_kernel(
 
         picked, look_words = {}, {}
 
-        def pick_words(g, h):
-            picked[g, h] = held([P, HALF], U32, "picked%d%d" % (g, h), "picked%d" % h)
-            at = (g * J + h * HALF) // 16
+        def pick_words(g, lo, width):
+            picked[g, lo] = held([P, width], U32, "picked%d_%d" % (g, lo), "picked_%d" % lo)
+            at = (g * J + lo) // 16
             nc.vector.tensor_copy(
-                out=picked[g, h][:], in_=table[:].bitcast(U32).indirect(offsets[:, at : at + HALF // 16])
+                out=picked[g, lo][:], in_=table[:].bitcast(U32).indirect(offsets[:, at : at + width // 16])
             )
 
-        def part_words(g, h):
-            look_words[g, h] = held([P, PASSES, 2 * HALF], U8, "parted%d%d" % (g, h))
+        def part_words(g, lo, width):
+            parted = held([P, PASSES, 2 * width], U8, "parted%d_%d" % (g, lo))
             nc.vector.tensor_copy(
-                out=look_words[g, h][:].bitcast(U16),
-                in_=picked[g, h][:].bitcast(U16).rearrange("p (j d) -> p d j", d=PASSES),
+                out=parted[:].bitcast(U16),
+                in_=picked[g, lo][:].bitcast(U16).rearrange("p (j d) -> p d j", d=PASSES),
             )
+            for part in range(width // CHUNK):
+                look_words[g, lo // CHUNK + part] = parted[:, :, 2 * CHUNK * part : 2 * CHUNK * (part + 1)]
 
         cast_w(0, 0, W0_SCALAR, "scalar")
         cast_w(0, W0_SCALAR, P, "vector")
         quant(w_codes[0][:], w_plane[0][:], w_bf[0][:])
-        pick_words(0, 0)
-        pick_words(0, 1)
-        part_words(0, 0)
-        pick_words(1, 0)
-        part_words(0, 1)
-        pick_words(1, 1)
-        part_words(1, 0)
+        pick_words(0, 0, HALF)
+        pick_words(0, HALF, HALF)
+        part_words(0, 0, HALF)
+        pick_words(1, 0, J)
+        part_words(0, HALF, HALF)
         cast_w(1, 0, W1_SCALAR, "scalar")
         cast_w(1, W1_SCALAR, P, "vector")
-        part_words(1, 1)
+        part_words(1, 0, J)
         quant(w_codes[1][:], w_plane[1][:], w_bf[1][:])
         wc_perm = held([P, PASSES, 2 * R], U8, "wc_perm")
 
@@ -204,7 +204,7 @@ def tile_list_pnet_bias_kernel(
             return lambda t: (
                 w_codes[a][:, P * t : P * (t + 1)].bitcast(FP8X4),
                 w_plane[a][:, P * t : P * (t + 1)],
-                look_words[g, q // 2][:, a, 2 * CHUNK * (q % 2) : 2 * CHUNK * (q % 2 + 1)].bitcast(FP4X4),
+                look_words[g, q][:, a, :].bitcast(FP4X4),
                 plane[:, a, at : at + CHUNK],
             )
 

@@ -276,12 +276,19 @@ def tile_list_pnet_bias_kernel(
             h_plane[q] = held([P, CHUNK], U8, "h_plane%d" % q)
             quant(h_codes[q][:], h_plane[q][:], hidden[q][:])
 
+        Y_SLOTS = {2: ((1, 2), (0, 0)), 3: ((0, 1), (0, 2))}
+
         def project(q):
-            y_bank = bank_tile([P, N // P, CHUNK], "y_bank", 0 if q == LAST else 1, q)
+            shared = q in Y_SLOTS
             result = held([P, N // P, CHUNK], F32, "result%d" % q)
+            if shared:
+                y = [bank_tile([P, CHUNK], "y_bank", *slot)[:] for slot in Y_SLOTS[q]]
+            else:
+                y_bank = bank_tile([P, N // P, CHUNK], "y_bank", 1, q)
+                y = [y_bank[:, s, :] for s in range(N // P)]
             for s in range(N // P):
                 nc.tensor.matmul_mx(
-                    out=y_bank[:, s, :],
+                    out=y[s],
                     lhsT=wd_raw[:, 2 * P * s : 2 * P * (s + 1)].bitcast(FP4X4),
                     lhsT_scale=wd_plane[:, P * s : P * (s + 1)],
                     rhs=h_codes[q][:].bitcast(FP8X4),
@@ -290,9 +297,10 @@ def tile_list_pnet_bias_kernel(
                     stop=True,
                 )
             for s in range(N // P):
-                nc.scalar.activation(
-                    out=result[:, s, :], in_=y_bank[:, s, :], func=ACT.Identity, bias=bias[:, s : s + 1]
-                )
+                if shared and s == 1:
+                    nc.vector.tensor_scalar_add(out=result[:, s, :], in0=y[s], scalar1=bias[:, s : s + 1])
+                else:
+                    nc.scalar.activation(out=result[:, s, :], in_=y[s], func=ACT.Identity, bias=bias[:, s : s + 1])
             nc.sync.dma_start(
                 out=out[:, CHUNK * q : CHUNK * (q + 1)].rearrange("(s p) j -> p s j", p=P), in_=result[:]
             )

@@ -21,14 +21,14 @@ PACK = 4
 PASSES = K // (P * PACK)
 LOOKS = 2
 CHUNK = 128
-CHUNKS = J // CHUNK
-LAST = CHUNKS - 1
 HALF = 2 * CHUNK
 ROWS = 32
 LOOK_AT, WC_AT, PLANE_W = 0, LOOKS * J, LOOKS * J + R
 
-W0_SCALAR = 64
-W1_SCALAR = 80
+W0_SCALAR = 28
+W1_SCALAR = 24
+RAW_BYTES = PACK * HALF * 4
+SLOTS = {"w_raw01": 0, "w_raw11": 1, "c_raw10": 2, "c_raw01": 3, "c_raw11": 4}
 
 
 def tile_list_pnet_bias_kernel(
@@ -37,10 +37,17 @@ def tile_list_pnet_bias_kernel(
     nc = tc.nc
     with ExitStack() as ctx:
         keep = ctx.enter_context(tc.tile_pool(name="keep", bufs=1))
+        shared = ctx.enter_context(tc.tile_pool(name="shared", bufs=1))
         psum = ctx.enter_context(tc.psum_pool(name="psum", bufs=1))
 
         def held(shape, dtype, name, tag=None):
             return keep.tile(shape, dtype, name=name, tag=tag or name, align_bytes=64)
+
+        def placed(shape, dtype, name, slot, at=0):
+            return shared.tile(shape, dtype, name=name, tag=name, align_bytes=64, offset=RAW_BYTES * slot + at)
+
+        def bank(shape, name, k):
+            return psum.tile(shape, F32, name=name, tag="bank%d" % k)
 
         offsets = keep.tile([P, LOOKS * J // 16], U16, name="offsets")
         nc.sync.dma_start(offsets[:], offs)
@@ -61,18 +68,21 @@ def tile_list_pnet_bias_kernel(
         nc.vector.memset(tab_rows[64:128, :].bitcast(I32), 0)
         nc.vector.memset(plane[:].rearrange("p a j -> p (a j)").bitcast(I32), 0)
 
-        def load_rows(src, a, lo, hi, name, tag=None):
-            raw = held([P, PACK, hi - lo], F32, name, tag)
-            rows = src[512 * a : 512 * (a + 1), lo:hi]
+        def load_rows(src, a, h, name):
+            if name in SLOTS:
+                raw = placed([P, PACK, HALF], F32, name, SLOTS[name])
+            else:
+                raw = held([P, PACK, HALF], F32, name)
+            rows = src[512 * a : 512 * (a + 1), HALF * h : HALF * (h + 1)]
             nc.sync.dma_start(out=raw[:], in_=rows.rearrange("(p i) n -> p i n", i=PACK))
             return raw
 
-        w_raw = {0: load_rows(w, 0, 0, R, "w_raw0")}
-        bias = held([P, N // P], F32, "bias")
-        with nc.allow_non_contiguous_dma(reason="one bias value a partition"):
-            nc.sync.dma_start(out=bias[:], in_=b.rearrange("(s p) -> p s", p=P))
         table = held([P, T], I32, "table")
         nc.sync.dma_start(out=table[:], in_=tab_words[0].rearrange("p t b -> p (t b)").bitcast(I32))
+        w_raw = {}
+        w_raw[0, 0] = load_rows(w, 0, 0, "w_raw00")
+        w_raw[0, 1] = load_rows(w, 0, 1, "w_raw01")
+        w_raw[1, 0] = load_rows(w, 1, 0, "w_raw10")
 
         picked_rows = held([P, LOOKS * J], U8, "picked_rows")
         nc.vector.tensor_copy(out=picked_rows[:], in_=tab_rows[:].indirect(offsets[:]))
@@ -89,13 +99,12 @@ def tile_list_pnet_bias_kernel(
                 in_=stage[8 * q : 8 * q + 8, :].bitcast(I32),
             )
 
-        w_raw[1] = load_rows(w, 1, 0, R, "w_raw1")
-        c_raw = {}
+        w_raw[1, 1] = load_rows(w, 1, 1, "w_raw11")
+        c_raw = {(0, 0): load_rows(c, 0, 0, "c_raw00")}
         wc_raw = held([P, PASSES, 2 * R], U8, "wc_raw")
         nc.sync.dma_start(out=wc_raw[:].bitcast(I32), in_=wc_words.bitcast(I32).rearrange("a p n -> p a n"))
-        c_raw[0] = load_rows(c, 0, 0, J, "c_raw0")
-        c_raw[1, 0] = load_rows(c, 1, 0, HALF, "c_raw1a")
-        c_raw[1, 1] = load_rows(c, 1, HALF, J, "c_raw1b")
+        for a, h in ((1, 0), (0, 1), (1, 1)):
+            c_raw[a, h] = load_rows(c, a, h, "c_raw%d%d" % (a, h))
         wd_raw = held([P, 2 * N], U8, "wd_raw")
         nc.sync.dma_start(out=wd_raw[:].bitcast(I32), in_=wd_words[0].bitcast(I32))
         wd_plane = held([P, N], U8, "wd_plane")
@@ -105,248 +114,236 @@ def tile_list_pnet_bias_kernel(
                 out=wd_plane[32 * q : 32 * q + 4, :].bitcast(I32),
                 in_=wd_scales[0, 4 * q : 4 * q + 4, :].bitcast(I32),
             )
+        bias = held([P, N // P], F32, "bias")
+        with nc.allow_non_contiguous_dma(reason="one bias value a partition"):
+            nc.sync.dma_start(out=bias[:], in_=b.rearrange("(s p) -> p s", p=P))
+
+        def round_copy(engine, dst, src):
+            if engine == "vector":
+                nc.vector.tensor_copy(out=dst, in_=src)
+            else:
+                nc.scalar.copy(out=dst, in_=src)
 
         w_bf = [held([P, PACK * R], BF16, "w_bf%d" % a) for a in range(PASSES)]
         w_codes = [held([P, R], U32, "w_codes%d" % a) for a in range(PASSES)]
         w_plane = [held([P, R], U8, "w_plane%d" % a) for a in range(PASSES)]
 
-        def round_copy(engine, dst, src):
-            if engine == "vector":
-                nc.vector.tensor_copy(out=dst, in_=src)
-            elif engine == "scalar":
-                nc.scalar.copy(out=dst, in_=src)
-            else:
-                nc.gpsimd.tensor_scalar(out=dst, in0=src, scalar1=1.0, scalar2=0.0, op0=ALU.mult, op1=ALU.add)
-
-        def cast_w(a, lo, hi, engine):
-            dst = w_bf[a][:].rearrange("p (t m i) -> p m i t", t=PACK, i=PACK)[:, lo:hi, :, :]
-            src = w_raw[a][:].rearrange("p i (m t) -> p m i t", t=PACK)[:, lo:hi, :, :]
+        def cast_w(a, h, lo, hi, engine):
+            dst = w_bf[a][:].rearrange("p (t m i) -> p m i t", t=PACK, i=PACK)[:, 64 * h + lo : 64 * h + hi, :, :]
+            src = w_raw[a, h][:].rearrange("p i (m t) -> p m i t", t=PACK)[:, lo:hi, :, :]
             round_copy(engine, dst, src)
 
         def quant(codes, scales, src):
             nc.vector.quantize_mx(out=codes.bitcast(FP8X4), scales=scales, in_=src)
 
-        picked, look_words = {}, {}
+        def quant_w(a):
+            for u in range(2):
+                cols = slice(2 * P * u, 2 * P * (u + 1))
+                quant(w_codes[a][:, cols], w_plane[a][:, cols], w_bf[a][:, PACK * cols.start : PACK * cols.stop])
 
-        def pick_words(g, lo, width):
-            picked[g, lo] = held([P, width], U32, "picked%d_%d" % (g, lo), "picked_%d" % lo)
-            at = (g * J + lo) // 16
+        def quantised(src, name):
+            width = src.shape[1] // PACK
+            codes = held([P, width], U32, name + "_codes")
+            scales = held([P, width], U8, name + "_plane")
+            quant(codes[:], scales[:], src)
+            return codes, scales
+
+        parted = {}
+
+        def pick_words(dst, g, h):
+            at = (g * J + h * HALF) // 16
+            nc.vector.tensor_copy(out=dst, in_=table[:].bitcast(U32).indirect(offsets[:, at : at + HALF // 16]))
+
+        def part_words(picked, g, h, dst):
             nc.vector.tensor_copy(
-                out=picked[g, lo][:], in_=table[:].bitcast(U32).indirect(offsets[:, at : at + width // 16])
+                out=dst[:].bitcast(U16), in_=picked[:].bitcast(U16).rearrange("p (j d) -> p d j", d=PASSES)
+            )
+            parted[g, h] = dst
+
+        def cast_c(dst, a, h, lo, width, engine):
+            round_copy(
+                engine,
+                dst.rearrange("p (n e i) -> p n i e", e=4, i=PACK),
+                c_raw[a, h][:, :, lo : lo + width].rearrange("p i (n e) -> p n i e", e=4),
             )
 
-        def part_words(g, lo, width):
-            parted = held([P, PASSES, 2 * width], U8, "parted%d_%d" % (g, lo))
-            nc.vector.tensor_copy(
-                out=parted[:].bitcast(U16),
-                in_=picked[g, lo][:].bitcast(U16).rearrange("p (j d) -> p d j", d=PASSES),
-            )
-            for part in range(width // CHUNK):
-                look_words[g, lo // CHUNK + part] = parted[:, :, 2 * CHUNK * part : 2 * CHUNK * (part + 1)]
-
-        cast_w(0, 0, W0_SCALAR, "scalar")
-        cast_w(0, W0_SCALAR, P, "vector")
-        quant(w_codes[0][:], w_plane[0][:], w_bf[0][:])
-        pick_words(0, 0, HALF)
-        pick_words(0, HALF, HALF)
-        part_words(0, 0, HALF)
-        pick_words(1, 0, J)
-        part_words(0, HALF, HALF)
-        cast_w(1, 0, W1_SCALAR, "scalar")
-        cast_w(1, W1_SCALAR, P, "vector")
-        part_words(1, 0, J)
-        quant(w_codes[1][:], w_plane[1][:], w_bf[1][:])
-        wc_perm = held([P, PASSES, 2 * R], U8, "wc_perm")
-
-        def deal_wc():
-            nc.vector.tensor_copy(
-                out=wc_perm[:].bitcast(U16).rearrange("p a (t m) -> p a t m", t=PACK),
-                in_=wc_raw[:].bitcast(U16).rearrange("p a (m t) -> p a t m", t=PACK),
+        def mx(dst, lhsT, lhsT_scale, rhs, rhs_scale, start, stop):
+            nc.tensor.matmul_mx(
+                out=dst, lhsT=lhsT, lhsT_scale=lhsT_scale, rhs=rhs, rhs_scale=rhs_scale, start=start, stop=stop
             )
 
-        c_bf, c_codes, c_plane = {}, {}, {}
-
-        def cast_c(a, q, width, raw, lo, engine):
-            c_bf[a, q] = held([P, PACK * width], BF16, "c_bf%d%d" % (a, q))
-            if engine == "gpsimd":
-                dst = c_bf[a, q][:].rearrange("p (n i) -> p n i", i=PACK)
-                src = raw[:, :, lo : lo + width].rearrange("p i n -> p n i")
-            else:
-                dst = c_bf[a, q][:].rearrange("p (n e i) -> p n i e", e=4, i=PACK)
-                src = raw[:, :, lo : lo + width].rearrange("p i (n e) -> p n i e", e=4)
-            round_copy(engine, dst, src)
-
-        def quant_c(a, q):
-            width = c_bf[a, q].shape[1] // PACK
-            codes = held([P, width], U32, "c_codes%d%d" % (a, q))
-            scales = held([P, width], U8, "c_plane%d%d" % (a, q))
-            quant(codes[:], scales[:], c_bf[a, q][:])
-            for part in range(width // CHUNK):
-                cols = slice(CHUNK * part, CHUNK * (part + 1))
-                c_codes[a, q + part] = codes[:, cols]
-                c_plane[a, q + part] = scales[:, cols]
-
-        def passes(bank, operands, start, stop):
-            for t in range(PACK):
-                lhsT, lhsT_scale, rhs, rhs_scale = operands(t)
-                nc.tensor.matmul_mx(
-                    out=bank[:, t, :],
-                    lhsT=lhsT,
-                    lhsT_scale=lhsT_scale,
-                    rhs=rhs,
-                    rhs_scale=rhs_scale,
-                    start=(start and t == 0),
-                    stop=(stop and t == PACK - 1),
+        def look(acc, slices, g, lo, width, a, start, stop):
+            at = LOOK_AT + J * g + lo
+            for k, t in enumerate(slices):
+                mx(
+                    acc[:, k, :],
+                    w_codes[a][:, P * t : P * (t + 1)].bitcast(FP8X4),
+                    w_plane[a][:, P * t : P * (t + 1)],
+                    parted[g, lo // HALF][:, a, 2 * (lo % HALF) : 2 * (lo % HALF + width)].bitcast(FP4X4),
+                    plane[:, a, at : at + width],
+                    start and k == 0,
+                    stop and k == len(slices) - 1,
                 )
 
-        def look_operands(g, q, a):
-            at = LOOK_AT + J * g + CHUNK * q
-            return lambda t: (
-                w_codes[a][:, P * t : P * (t + 1)].bitcast(FP8X4),
-                w_plane[a][:, P * t : P * (t + 1)],
-                look_words[g, q][:, a, :].bitcast(FP4X4),
-                plane[:, a, at : at + CHUNK],
-            )
+        def own(acc, slices, a, c_mx, lo, width, start, stop):
+            for k, t in enumerate(slices):
+                mx(
+                    acc[:, k, :],
+                    wc_perm[:, a, 2 * P * t : 2 * P * (t + 1)].bitcast(FP4X4),
+                    plane[:, a, WC_AT + P * t : WC_AT + P * (t + 1)],
+                    c_mx[0][:, lo : lo + width].bitcast(FP8X4),
+                    c_mx[1][:, lo : lo + width],
+                    start and k == 0,
+                    stop and k == len(slices) - 1,
+                )
 
-        def own_operands(q, a):
-            return lambda t: (
-                wc_perm[:, a, 2 * P * t : 2 * P * (t + 1)].bitcast(FP4X4),
-                plane[:, a, WC_AT + P * t : WC_AT + P * (t + 1)],
-                c_codes[a, q].bitcast(FP8X4),
-                c_plane[a, q],
-            )
+        def woven(acc):
+            return acc[:].rearrange("p t j -> p j t")
 
-        def bank_tile(shape, name, g, q):
-            return psum.tile(shape, F32, name=name, tag="bank%d%d" % (g, q))
-
-        def woven(bank):
-            return bank[:].rearrange("p t j -> p j t")
-
-        look_bank = {}
-        for g in range(LOOKS):
-            for q in range(CHUNKS):
-                look_bank[g, q] = bank_tile([P, PACK, CHUNK], "look_bank", g, q)
-        for g in range(LOOKS):
-            for q in range(CHUNKS):
-                passes(look_bank[g, q], look_operands(g, q, 0), True, False)
-        for q in range(CHUNKS):
-            for g in range(LOOKS):
-                passes(look_bank[g, q], look_operands(g, q, 1), False, q != LAST)
-
-        first, pooled, own_bank, summed, hidden, h_codes, h_plane = {}, {}, {}, {}, {}, {}, {}
-
-        def copy_first(q):
-            first[q] = held([P, CHUNK, PACK], F32, "first%d" % q)
-            if q == LAST:
-                nc.scalar.activation(out=first[q][:], in_=woven(look_bank[0, q]), func=ACT.Relu)
-            else:
-                nc.scalar.copy(out=first[q][:], in_=woven(look_bank[0, q]))
-
-        def pool_pair(q):
-            if q == LAST:
-                hidden[q] = held([P, CHUNK * PACK], BF16, "hidden%d" % q)
-                dst = hidden[q][:].rearrange("p (j t) -> p j t", t=PACK)
-            else:
-                pooled[q] = held([P, CHUNK, PACK], F32, "pooled%d" % q)
-                dst = pooled[q][:]
-            nc.vector.tensor_tensor(out=dst, in0=woven(look_bank[1, q]), in1=first[q][:], op=ALU.max)
-
-        def own(q, a):
-            if a == 0:
-                own_bank[q] = bank_tile([P, PACK, CHUNK], "own_bank", 0, q)
-            passes(own_bank[q], own_operands(q, a), a == 0, a == PASSES - 1)
-
-        def own_joint(g, a):
-            passes(look_bank[g, LAST], own_operands(LAST, a), False, a == PASSES - 1)
-
-        def add_own(q):
-            summed[q] = held([P, CHUNK, PACK], BF16, "summed%d" % q)
-            nc.vector.tensor_tensor(out=summed[q][:], in0=woven(own_bank[q]), in1=pooled[q][:], op=ALU.add)
-
-        def relu(q):
-            hidden[q] = held([P, CHUNK * PACK], BF16, "hidden%d" % q)
-            flat = summed[q][:].rearrange("p j t -> p (j t)")
-            if q in (0,):
-                nc.scalar.activation(out=hidden[q][:], in_=flat, func=ACT.Relu)
-            else:
-                nc.vector.tensor_scalar_max(out=hidden[q][:], in0=flat, scalar1=0.0)
-
-        def quant_h(q):
-            h_codes[q] = held([P, CHUNK], U32, "h_codes%d" % q)
-            h_plane[q] = held([P, CHUNK], U8, "h_plane%d" % q)
-            quant(h_codes[q][:], h_plane[q][:], hidden[q][:])
-
-        Y_SLOTS = {2: ((1, 2), (0, 0)), 3: ((0, 1), (0, 2))}
-
-        def project(q):
-            shared = q in Y_SLOTS
-            result = held([P, N // P, CHUNK], F32, "result%d" % q)
-            if shared:
-                y = [bank_tile([P, CHUNK], "y_bank", *slot)[:] for slot in Y_SLOTS[q]]
-            else:
-                y_bank = bank_tile([P, N // P, CHUNK], "y_bank", 1, q)
-                y = [y_bank[:, s, :] for s in range(N // P)]
+        def project(h_mx, lo, width, y, engines, name):
+            result = held([P, N // P, width], F32, name)
             for s in range(N // P):
-                nc.tensor.matmul_mx(
-                    out=y[s],
-                    lhsT=wd_raw[:, 2 * P * s : 2 * P * (s + 1)].bitcast(FP4X4),
-                    lhsT_scale=wd_plane[:, P * s : P * (s + 1)],
-                    rhs=h_codes[q][:].bitcast(FP8X4),
-                    rhs_scale=h_plane[q][:],
-                    start=True,
-                    stop=True,
+                mx(
+                    y[s],
+                    wd_raw[:, 2 * P * s : 2 * P * (s + 1)].bitcast(FP4X4),
+                    wd_plane[:, P * s : P * (s + 1)],
+                    h_mx[0][:].bitcast(FP8X4),
+                    h_mx[1][:],
+                    True,
+                    True,
                 )
             for s in range(N // P):
-                if shared and s == 1:
+                if engines[s] == "vector":
                     nc.vector.tensor_scalar_add(out=result[:, s, :], in0=y[s], scalar1=bias[:, s : s + 1])
                 else:
                     nc.scalar.activation(out=result[:, s, :], in_=y[s], func=ACT.Identity, bias=bias[:, s : s + 1])
-            nc.sync.dma_start(
-                out=out[:, CHUNK * q : CHUNK * (q + 1)].rearrange("(s p) j -> p s j", p=P), in_=result[:]
-            )
+            nc.sync.dma_start(out=out[:, lo : lo + width].rearrange("(s p) j -> p s j", p=P), in_=result[:])
 
-        deal_wc()
-        copy_first(0)
-        cast_c(0, 0, 256, c_raw[0], 0, "vector")
-        cast_c(0, 2, 256, c_raw[0], 256, "vector")
-        copy_first(1)
-        quant_c(0, 0)
-        pool_pair(0)
-        quant_c(0, 2)
-        copy_first(2)
-        pool_pair(1)
-        own(0, 0)
-        own(1, 0)
-        cast_c(1, 0, 128, c_raw[1, 0], 0, "scalar")
-        quant_c(1, 0)
-        pool_pair(2)
-        own(2, 0)
-        own(0, 1)
-        cast_c(1, 1, 128, c_raw[1, 0], 128, "scalar")
-        quant_c(1, 1)
-        own_joint(0, 0)
-        own_joint(1, 0)
-        own(1, 1)
-        add_own(0)
-        cast_c(1, 2, 128, c_raw[1, 1], 0, "scalar")
-        cast_c(1, 3, 128, c_raw[1, 1], 128, "scalar")
-        quant_c(1, 2)
-        quant_c(1, 3)
-        own(2, 1)
-        own_joint(0, 1)
-        own_joint(1, 1)
-        add_own(1)
-        relu(0)
-        add_own(2)
-        copy_first(3)
-        relu(1)
-        quant_h(0)
-        quant_h(1)
-        project(0)
-        project(1)
-        relu(2)
-        pool_pair(3)
-        quant_h(2)
-        quant_h(3)
-        project(2)
-        project(3)
+        PAIRS = ((0, 1), (2, 3))
+        ALL = (0, 1, 2, 3)
+
+        picked_a = [held([P, HALF], U32, "picked_a%d" % g) for g in range(LOOKS)]
+        for g in range(LOOKS):
+            pick_words(picked_a[g][:], g, 0)
+        for g in range(LOOKS):
+            part_words(picked_a[g], g, 0, held([P, PASSES, 2 * HALF], U8, "parted_a%d" % g))
+        cast_w(0, 0, 0, 64, "scalar")
+        cast_w(0, 1, 0, W0_SCALAR, "scalar")
+        cast_w(0, 1, W0_SCALAR, 64, "vector")
+        picked_b = [held([P, HALF], U32, "picked_b0")]
+        pick_words(picked_b[0][:], 0, 1)
+        quant_w(0)
+        pair_look = {}
+        for g in range(LOOKS):
+            for u in range(2):
+                pair_look[g, u] = bank([P, 2, HALF], "pair_look", 2 * u + g)
+                look(pair_look[g, u], PAIRS[u], g, 0, HALF, 0, True, False)
+        picked_b.append(placed([P, HALF], U32, "picked_b1", SLOTS["w_raw01"]))
+        pick_words(picked_b[1][:], 1, 1)
+        for g in range(LOOKS):
+            dst = placed([P, PASSES, 2 * HALF], U8, "parted_b%d" % g, SLOTS["w_raw01"], 1024 * (g + 1))
+            part_words(picked_b[g], g, 1, dst)
+        look2 = [bank([P, PACK, CHUNK], "look2", 4 + g) for g in range(LOOKS)]
+        look(look2[0], ALL, 0, 2 * CHUNK, CHUNK, 0, True, False)
+        cast_w(1, 0, 0, 64, "scalar")
+        cast_w(1, 1, 0, W1_SCALAR, "scalar")
+        cast_w(1, 1, W1_SCALAR, 64, "vector")
+        quant_w(1)
+        for g in range(LOOKS):
+            for u in range(2):
+                look(pair_look[g, u], PAIRS[u], g, 0, HALF, 1, False, True)
+
+        wide = PACK * CHUNK
+        c_bf = {(0, 0): placed([P, 2 * wide], BF16, "c_bf00", SLOTS["w_raw11"])}
+
+        def cast_chunk(a, q, engine):
+            h, k = divmod(q, 2)
+            cast_c(c_bf[a, h][:, wide * k : wide * (k + 1)], a, h, CHUNK * k, CHUNK, engine)
+
+        cast_chunk(0, 0, "vector")
+        cast_chunk(0, 1, "scalar")
+        wc_perm = placed([P, PASSES, 2 * R], U8, "wc_perm", SLOTS["w_raw11"], 2048)
+        nc.vector.tensor_copy(
+            out=wc_perm[:].bitcast(U16).rearrange("p a (t m) -> p a t m", t=PACK),
+            in_=wc_raw[:].bitcast(U16).rearrange("p a (m t) -> p a t m", t=PACK),
+        )
+
+        def copy_first(acc, name, relu):
+            first = held([P, acc.shape[2], acc.shape[1]], F32, name)
+            if relu:
+                nc.scalar.activation(out=first[:], in_=woven(acc), func=ACT.Relu)
+            else:
+                nc.scalar.copy(out=first[:], in_=woven(acc))
+            return first
+
+        def join(dst, acc, other, op):
+            nc.vector.tensor_tensor(out=dst, in0=woven(acc), in1=other[:], op=op)
+
+        def pooled(acc, first, name):
+            dst = held(list(first.shape), F32, name)
+            join(dst[:], acc, first, ALU.max)
+            return dst
+
+        c00 = quantised(c_bf[0, 0][:], "c00")
+        first_a = [copy_first(pair_look[0, u], "first_a%d" % u, False) for u in range(2)]
+        look(look2[0], ALL, 0, 2 * CHUNK, CHUNK, 1, False, True)
+        look(look2[1], ALL, 1, 2 * CHUNK, CHUNK, 1, True, False)
+        look(look2[1], ALL, 1, 2 * CHUNK, CHUNK, 0, False, True)
+        pooled_a = [pooled(pair_look[1, 0], first_a[0], "pooled_a0")]
+        c_bf[1, 0] = held([P, 2 * wide], BF16, "c_bf10", "parted_a0")
+        cast_chunk(1, 0, "vector")
+        cast_chunk(1, 1, "scalar")
+        pooled_a.append(pooled(pair_look[1, 1], first_a[1], "pooled_a1"))
+        own_a = [bank([P, 2, HALF], "own_a", 2 * u) for u in range(2)]
+        for u in range(2):
+            own(own_a[u], PAIRS[u], 0, c00, 0, HALF, True, False)
+        c10 = quantised(c_bf[1, 0][:], "c10")
+        for u in range(2):
+            own(own_a[u], PAIRS[u], 1, c10, 0, HALF, False, True)
+        joint = [bank([P, PACK, CHUNK], "joint", 6 + g) for g in range(LOOKS)]
+        for g in range(LOOKS):
+            look(joint[g], ALL, g, 3 * CHUNK, CHUNK, 1, True, False)
+            look(joint[g], ALL, g, 3 * CHUNK, CHUNK, 0, False, False)
+        first2 = copy_first(look2[0], "first2", False)
+        c_bf[0, 1] = placed([P, 2 * wide], BF16, "c_bf01", SLOTS["c_raw10"])
+        cast_chunk(0, 2, "vector")
+        cast_chunk(0, 3, "scalar")
+        pooled2 = pooled(look2[1], first2, "pooled2")
+        c01 = quantised(c_bf[0, 1][:], "c01")
+        own2 = bank([P, PACK, CHUNK], "own2", 4)
+        own(own2, ALL, 0, c01, 0, CHUNK, True, False)
+        own(joint[0], ALL, 0, c01, CHUNK, CHUNK, False, False)
+        summed_a = held([P, 2, HALF, 2], BF16, "summed_a")
+        join(summed_a[:, 0, :, :], own_a[0], pooled_a[0], ALU.add)
+        c_bf[1, 1] = placed([P, 2 * wide], BF16, "c_bf11", SLOTS["c_raw01"])
+        cast_chunk(1, 2, "scalar")
+        cast_chunk(1, 3, "scalar")
+        c12 = quantised(c_bf[1, 1][:, 0:wide], "c12")
+        own(own2, ALL, 1, c12, 0, CHUNK, False, True)
+        own(joint[1], ALL, 0, c01, CHUNK, CHUNK, False, False)
+        join(summed_a[:, 1, :, :], own_a[1], pooled_a[1], ALU.add)
+        c13 = quantised(c_bf[1, 1][:, wide : 2 * wide], "c13")
+        for g in range(LOOKS):
+            own(joint[g], ALL, 1, c13, 0, CHUNK, False, True)
+        summed2 = held([P, CHUNK, PACK], BF16, "summed2")
+        join(summed2[:], own2, pooled2, ALU.add)
+        hidden_a = placed([P, HALF * PACK], BF16, "hidden_a", SLOTS["c_raw11"])
+        nc.vector.tensor_scalar_max(
+            out=hidden_a[:].rearrange("p (j u e) -> p j u e", u=2, e=2),
+            in0=summed_a[:].rearrange("p u j e -> p j u e"),
+            scalar1=0.0,
+        )
+        hidden2 = held([P, CHUNK * PACK], BF16, "hidden2")
+        nc.vector.tensor_scalar_max(out=hidden2[:], in0=summed2[:].rearrange("p j t -> p (j t)"), scalar1=0.0)
+        h_a = quantised(hidden_a[:], "h_a")
+        first3 = copy_first(joint[0], "first3", True)
+        y_a = bank([P, N // P, HALF], "y_a", 1)
+        project(h_a, 0, HALF, [y_a[:, s, :] for s in range(N // P)], ("scalar", "scalar"), "result_a")
+        h2 = quantised(hidden2[:], "h2")
+        y2 = [bank([P, CHUNK], "y2", k)[:] for k in (0, 2)]
+        hidden3 = held([P, CHUNK, PACK], BF16, "hidden3")
+        join(hidden3[:], joint[1], first3, ALU.max)
+        h3 = quantised(hidden3[:].rearrange("p j t -> p (j t)"), "h3")
+        project(h2, 2 * CHUNK, CHUNK, y2, ("scalar", "vector"), "result2")
+        y3 = [bank([P, CHUNK], "y3", k)[:] for k in (3, 5)]
+        project(h3, 3 * CHUNK, CHUNK, y3, ("scalar", "vector"), "result3")

@@ -21,14 +21,15 @@ PACK = 4
 PASSES = K // (P * PACK)
 LOOKS = 2
 CHUNK = 128
+CHUNKS = J // CHUNK
+LAST = CHUNKS - 1
 HALF = 2 * CHUNK
 ROWS = 32
 LOOK_AT, WC_AT, PLANE_W = 0, LOOKS * J, LOOKS * J + R
 
-W0_SCALAR = 28
-W1_SCALAR = 24
-RAW_BYTES = PACK * HALF * 4
-SLOTS = {"w_raw01": 0, "w_raw11": 1, "c_raw10": 2, "c_raw01": 3, "c_raw11": 4}
+W0_SCALAR = 64
+W1_SCALAR = 76
+RAW = PACK * R * 4
 
 
 def tile_list_pnet_bias_kernel(
@@ -43,11 +44,8 @@ def tile_list_pnet_bias_kernel(
         def held(shape, dtype, name, tag=None):
             return keep.tile(shape, dtype, name=name, tag=tag or name, align_bytes=64)
 
-        def placed(shape, dtype, name, slot, at=0):
-            return shared.tile(shape, dtype, name=name, tag=name, align_bytes=64, offset=RAW_BYTES * slot + at)
-
-        def bank(shape, name, k):
-            return psum.tile(shape, F32, name=name, tag="bank%d" % k)
+        def placed(shape, dtype, name, at):
+            return shared.tile(shape, dtype, name=name, tag=name, align_bytes=64, offset=at)
 
         offsets = keep.tile([P, LOOKS * J // 16], U16, name="offsets")
         nc.sync.dma_start(offsets[:], offs)
@@ -68,21 +66,16 @@ def tile_list_pnet_bias_kernel(
         nc.vector.memset(tab_rows[64:128, :].bitcast(I32), 0)
         nc.vector.memset(plane[:].rearrange("p a j -> p (a j)").bitcast(I32), 0)
 
-        def load_rows(src, a, h, name):
-            if name in SLOTS:
-                raw = placed([P, PACK, HALF], F32, name, SLOTS[name])
-            else:
-                raw = held([P, PACK, HALF], F32, name)
-            rows = src[512 * a : 512 * (a + 1), HALF * h : HALF * (h + 1)]
+        def load_rows(src, a, lo, hi, name, at=None):
+            shape = [P, PACK, hi - lo]
+            raw = held(shape, F32, name) if at is None else placed(shape, F32, name, at)
+            rows = src[512 * a : 512 * (a + 1), lo:hi]
             nc.sync.dma_start(out=raw[:], in_=rows.rearrange("(p i) n -> p i n", i=PACK))
             return raw
 
+        w_raw = {0: load_rows(w, 0, 0, R, "w_raw0", 0)}
         table = held([P, T], I32, "table")
         nc.sync.dma_start(out=table[:], in_=tab_words[0].rearrange("p t b -> p (t b)").bitcast(I32))
-        w_raw = {}
-        w_raw[0, 0] = load_rows(w, 0, 0, "w_raw00")
-        w_raw[0, 1] = load_rows(w, 0, 1, "w_raw01")
-        w_raw[1, 0] = load_rows(w, 1, 0, "w_raw10")
 
         picked_rows = held([P, LOOKS * J], U8, "picked_rows")
         nc.vector.tensor_copy(out=picked_rows[:], in_=tab_rows[:].indirect(offsets[:]))
@@ -99,12 +92,12 @@ def tile_list_pnet_bias_kernel(
                 in_=stage[8 * q : 8 * q + 8, :].bitcast(I32),
             )
 
-        w_raw[1, 1] = load_rows(w, 1, 1, "w_raw11")
-        c_raw = {(0, 0): load_rows(c, 0, 0, "c_raw00")}
+        w_raw[1] = load_rows(w, 1, 0, R, "w_raw1", RAW)
+        c_raw = {0: load_rows(c, 0, 0, J, "c_raw0")}
         wc_raw = held([P, PASSES, 2 * R], U8, "wc_raw")
         nc.sync.dma_start(out=wc_raw[:].bitcast(I32), in_=wc_words.bitcast(I32).rearrange("a p n -> p a n"))
-        for a, h in ((1, 0), (0, 1), (1, 1)):
-            c_raw[a, h] = load_rows(c, a, h, "c_raw%d%d" % (a, h))
+        c_raw[1, 0] = load_rows(c, 1, 0, HALF, "c_raw1a")
+        c_raw[1, 1] = load_rows(c, 1, HALF, J, "c_raw1b")
         wd_raw = held([P, 2 * N], U8, "wd_raw")
         nc.sync.dma_start(out=wd_raw[:].bitcast(I32), in_=wd_words[0].bitcast(I32))
         wd_plane = held([P, N], U8, "wd_plane")
@@ -118,232 +111,254 @@ def tile_list_pnet_bias_kernel(
         with nc.allow_non_contiguous_dma(reason="one bias value a partition"):
             nc.sync.dma_start(out=bias[:], in_=b.rearrange("(s p) -> p s", p=P))
 
+        w_bf = [held([P, PACK * R], BF16, "w_bf%d" % a) for a in range(PASSES)]
+        w_codes = [held([P, R], U32, "w_codes%d" % a) for a in range(PASSES)]
+        w_plane = [held([P, R], U8, "w_plane%d" % a) for a in range(PASSES)]
+
         def round_copy(engine, dst, src):
             if engine == "vector":
                 nc.vector.tensor_copy(out=dst, in_=src)
             else:
                 nc.scalar.copy(out=dst, in_=src)
 
-        w_bf = [held([P, PACK * R], BF16, "w_bf%d" % a) for a in range(PASSES)]
-        w_codes = [held([P, R], U32, "w_codes%d" % a) for a in range(PASSES)]
-        w_plane = [held([P, R], U8, "w_plane%d" % a) for a in range(PASSES)]
-
-        def cast_w(a, h, lo, hi, engine):
-            dst = w_bf[a][:].rearrange("p (t m i) -> p m i t", t=PACK, i=PACK)[:, 64 * h + lo : 64 * h + hi, :, :]
-            src = w_raw[a, h][:].rearrange("p i (m t) -> p m i t", t=PACK)[:, lo:hi, :, :]
+        def cast_w(a, lo, hi, engine):
+            dst = w_bf[a][:].rearrange("p (t m i) -> p m i t", t=PACK, i=PACK)[:, lo:hi, :, :]
+            src = w_raw[a][:].rearrange("p i (m t) -> p m i t", t=PACK)[:, lo:hi, :, :]
             round_copy(engine, dst, src)
 
         def quant(codes, scales, src):
             nc.vector.quantize_mx(out=codes.bitcast(FP8X4), scales=scales, in_=src)
 
-        def quant_w(a):
-            for u in range(2):
-                cols = slice(2 * P * u, 2 * P * (u + 1))
-                quant(w_codes[a][:, cols], w_plane[a][:, cols], w_bf[a][:, PACK * cols.start : PACK * cols.stop])
+        picked, look_words = {}, {}
 
-        def quantised(src, name):
-            width = src.shape[1] // PACK
-            codes = held([P, width], U32, name + "_codes")
-            scales = held([P, width], U8, name + "_plane")
-            quant(codes[:], scales[:], src)
-            return codes, scales
-
-        parted = {}
-
-        def pick_words(dst, g, h):
-            at = (g * J + h * HALF) // 16
-            nc.vector.tensor_copy(out=dst, in_=table[:].bitcast(U32).indirect(offsets[:, at : at + HALF // 16]))
-
-        def part_words(picked, g, h, dst):
+        def pick_words(g, lo, width, at):
+            picked[g, lo] = placed([P, width], U32, "picked%d_%d" % (g, lo), at)
+            at = (g * J + lo) // 16
             nc.vector.tensor_copy(
-                out=dst[:].bitcast(U16), in_=picked[:].bitcast(U16).rearrange("p (j d) -> p d j", d=PASSES)
-            )
-            parted[g, h] = dst
-
-        def cast_c(dst, a, h, lo, width, engine):
-            round_copy(
-                engine,
-                dst.rearrange("p (n e i) -> p n i e", e=4, i=PACK),
-                c_raw[a, h][:, :, lo : lo + width].rearrange("p i (n e) -> p n i e", e=4),
+                out=picked[g, lo][:], in_=table[:].bitcast(U32).indirect(offsets[:, at : at + width // 16])
             )
 
-        def mx(dst, lhsT, lhsT_scale, rhs, rhs_scale, start, stop):
-            nc.tensor.matmul_mx(
-                out=dst, lhsT=lhsT, lhsT_scale=lhsT_scale, rhs=rhs, rhs_scale=rhs_scale, start=start, stop=stop
+        def part_words(g, lo, width):
+            parted = held([P, PASSES, 2 * width], U8, "parted%d_%d" % (g, lo))
+            nc.vector.tensor_copy(
+                out=parted[:].bitcast(U16),
+                in_=picked[g, lo][:].bitcast(U16).rearrange("p (j d) -> p d j", d=PASSES),
+            )
+            for part in range(width // CHUNK):
+                look_words[g, lo // CHUNK + part] = parted[:, :, 2 * CHUNK * part : 2 * CHUNK * (part + 1)]
+
+        cast_w(0, 0, W0_SCALAR, "scalar")
+        cast_w(0, W0_SCALAR, P, "vector")
+        quant(w_codes[0][:], w_plane[0][:], w_bf[0][:])
+        pick_words(0, 0, CHUNK, 0)
+        pick_words(0, CHUNK, CHUNK, 2048 - 256)
+        part_words(0, 0, CHUNK)
+        part_words(0, CHUNK, CHUNK)
+        pick_words(0, HALF, HALF, 0)
+        pick_words(1, 0, HALF, 1024)
+        pick_words(1, HALF, HALF, 2048)
+        part_words(0, HALF, HALF)
+        part_words(1, 0, HALF)
+        part_words(1, HALF, HALF)
+        cast_w(1, 0, W1_SCALAR, "scalar")
+        cast_w(1, W1_SCALAR, P, "vector")
+        for u in range(2):
+            cols = slice(2 * P * u, 2 * P * (u + 1))
+            quant(w_codes[1][:, cols], w_plane[1][:, cols], w_bf[1][:, PACK * cols.start : PACK * cols.stop])
+        wc_perm = placed([P, PASSES, 2 * R], U8, "wc_perm", RAW + 4096)
+
+        def deal_wc():
+            nc.vector.tensor_copy(
+                out=wc_perm[:].bitcast(U16).rearrange("p a (t m) -> p a t m", t=PACK),
+                in_=wc_raw[:].bitcast(U16).rearrange("p a (m t) -> p a t m", t=PACK),
             )
 
-        def look(acc, slices, g, lo, width, a, start, stop):
-            at = LOOK_AT + J * g + lo
-            for k, t in enumerate(slices):
-                mx(
-                    acc[:, k, :],
-                    w_codes[a][:, P * t : P * (t + 1)].bitcast(FP8X4),
-                    w_plane[a][:, P * t : P * (t + 1)],
-                    parted[g, lo // HALF][:, a, 2 * (lo % HALF) : 2 * (lo % HALF + width)].bitcast(FP4X4),
-                    plane[:, a, at : at + width],
-                    start and k == 0,
-                    stop and k == len(slices) - 1,
+        c_bf, c_codes, c_plane = {}, {}, {}
+
+        def cast_c(a, q, width, raw, lo, engine, at=0, whole=None):
+            shape, name = [P, PACK * (whole or width)], "c_bf%d%d" % (a, q)
+            if at == 0 and a == 0:
+                c_bf[a, q] = placed(shape, BF16, name, RAW + 1024 * q)
+            elif at == 0:
+                c_bf[a, q] = held(shape, BF16, name)
+            dst = c_bf[a, q][:, PACK * at : PACK * (at + width)].rearrange("p (n e i) -> p n i e", e=4, i=PACK)
+            src = raw[:, :, lo : lo + width].rearrange("p i (n e) -> p n i e", e=4)
+            round_copy(engine, dst, src)
+
+        def quant_c(a, q):
+            width = c_bf[a, q].shape[1] // PACK
+            codes = held([P, width], U32, "c_codes%d%d" % (a, q))
+            scales = held([P, width], U8, "c_plane%d%d" % (a, q))
+            quant(codes[:], scales[:], c_bf[a, q][:])
+            for part in range(width // CHUNK):
+                cols = slice(CHUNK * part, CHUNK * (part + 1))
+                c_codes[a, q + part] = codes[:, cols]
+                c_plane[a, q + part] = scales[:, cols]
+
+        def passes(bank, operands, start, stop):
+            for t in range(PACK):
+                lhsT, lhsT_scale, rhs, rhs_scale = operands(t)
+                nc.tensor.matmul_mx(
+                    out=bank[:, t, :],
+                    lhsT=lhsT,
+                    lhsT_scale=lhsT_scale,
+                    rhs=rhs,
+                    rhs_scale=rhs_scale,
+                    start=(start and t == 0),
+                    stop=(stop and t == PACK - 1),
                 )
 
-        def own(acc, slices, a, c_mx, lo, width, start, stop):
-            for k, t in enumerate(slices):
-                mx(
-                    acc[:, k, :],
-                    wc_perm[:, a, 2 * P * t : 2 * P * (t + 1)].bitcast(FP4X4),
-                    plane[:, a, WC_AT + P * t : WC_AT + P * (t + 1)],
-                    c_mx[0][:, lo : lo + width].bitcast(FP8X4),
-                    c_mx[1][:, lo : lo + width],
-                    start and k == 0,
-                    stop and k == len(slices) - 1,
-                )
+        def look_operands(g, q, a):
+            at = LOOK_AT + J * g + CHUNK * q
+            return lambda t: (
+                w_codes[a][:, P * t : P * (t + 1)].bitcast(FP8X4),
+                w_plane[a][:, P * t : P * (t + 1)],
+                look_words[g, q][:, a, :].bitcast(FP4X4),
+                plane[:, a, at : at + CHUNK],
+            )
 
-        def woven(acc):
-            return acc[:].rearrange("p t j -> p j t")
+        def own_operands(q, a):
+            return lambda t: (
+                wc_perm[:, a, 2 * P * t : 2 * P * (t + 1)].bitcast(FP4X4),
+                plane[:, a, WC_AT + P * t : WC_AT + P * (t + 1)],
+                c_codes[a, q].bitcast(FP8X4),
+                c_plane[a, q],
+            )
 
-        def project(h_mx, lo, width, y, engines, name):
-            result = held([P, N // P, width], F32, name)
+        def bank_tile(shape, name, g, q):
+            return psum.tile(shape, F32, name=name, tag="bank%d%d" % (g, q))
+
+        def woven(bank):
+            return bank[:].rearrange("p t j -> p j t")
+
+        look_bank = {}
+        for g in range(LOOKS):
+            for q in range(CHUNKS):
+                look_bank[g, q] = bank_tile([P, PACK, CHUNK], "look_bank", g, q)
+        for g in range(LOOKS):
+            for q in range(CHUNKS):
+                passes(look_bank[g, q], look_operands(g, q, 0), True, False)
+        for q in range(LAST):
+            for g in range(LOOKS):
+                passes(look_bank[g, q], look_operands(g, q, 1), False, True)
+
+        first, pooled, own_bank, summed, hidden, h_codes, h_plane = {}, {}, {}, {}, {}, {}, {}
+
+        def copy_first(q):
+            first[q] = held([P, CHUNK, PACK], F32, "first%d" % q)
+            if q == LAST:
+                nc.scalar.activation(out=first[q][:], in_=woven(look_bank[0, q]), func=ACT.Relu)
+            else:
+                nc.scalar.copy(out=first[q][:], in_=woven(look_bank[0, q]))
+
+        def pool_pair(q):
+            if q == LAST:
+                hidden[q] = held([P, CHUNK * PACK], BF16, "hidden%d" % q)
+                dst = hidden[q][:].rearrange("p (j t) -> p j t", t=PACK)
+            else:
+                pooled[q] = held([P, CHUNK, PACK], F32, "pooled%d" % q)
+                dst = pooled[q][:]
+            nc.vector.tensor_tensor(out=dst, in0=woven(look_bank[1, q]), in1=first[q][:], op=ALU.max)
+
+        def own(q, a):
+            if a == 0:
+                own_bank[q] = bank_tile([P, PACK, CHUNK], "own_bank", 0, q)
+            passes(own_bank[q], own_operands(q, a), a == 0, a == PASSES - 1)
+
+        def own_joint(g, a):
+            passes(look_bank[g, LAST], own_operands(LAST, a), False, a == PASSES - 1)
+
+        def add_own(q):
+            summed[q] = held([P, CHUNK, PACK], BF16, "summed%d" % q)
+            nc.vector.tensor_tensor(out=summed[q][:], in0=woven(own_bank[q]), in1=pooled[q][:], op=ALU.add)
+
+        def relu(q):
+            hidden[q] = held([P, CHUNK * PACK], BF16, "hidden%d" % q)
+            flat = summed[q][:].rearrange("p j t -> p (j t)")
+            if q in (0,):
+                nc.scalar.activation(out=hidden[q][:], in_=flat, func=ACT.Relu)
+            else:
+                nc.vector.tensor_scalar_max(out=hidden[q][:], in0=flat, scalar1=0.0)
+
+        def quant_h(q):
+            h_codes[q] = held([P, CHUNK], U32, "h_codes%d" % q)
+            h_plane[q] = held([P, CHUNK], U8, "h_plane%d" % q)
+            quant(h_codes[q][:], h_plane[q][:], hidden[q][:])
+
+        Y_SLOTS = {2: ((1, 2), (0, 0)), 3: ((0, 1), (0, 2))}
+
+        def project(q):
+            shared = q in Y_SLOTS
+            result = held([P, N // P, CHUNK], F32, "result%d" % q)
+            if shared:
+                y = [bank_tile([P, CHUNK], "y_bank", *slot)[:] for slot in Y_SLOTS[q]]
+            else:
+                y_bank = bank_tile([P, N // P, CHUNK], "y_bank", 1, q)
+                y = [y_bank[:, s, :] for s in range(N // P)]
             for s in range(N // P):
-                mx(
-                    y[s],
-                    wd_raw[:, 2 * P * s : 2 * P * (s + 1)].bitcast(FP4X4),
-                    wd_plane[:, P * s : P * (s + 1)],
-                    h_mx[0][:].bitcast(FP8X4),
-                    h_mx[1][:],
-                    True,
-                    True,
+                nc.tensor.matmul_mx(
+                    out=y[s],
+                    lhsT=wd_raw[:, 2 * P * s : 2 * P * (s + 1)].bitcast(FP4X4),
+                    lhsT_scale=wd_plane[:, P * s : P * (s + 1)],
+                    rhs=h_codes[q][:].bitcast(FP8X4),
+                    rhs_scale=h_plane[q][:],
+                    start=True,
+                    stop=True,
                 )
             for s in range(N // P):
-                if engines[s] == "vector":
+                if shared and s == 1:
                     nc.vector.tensor_scalar_add(out=result[:, s, :], in0=y[s], scalar1=bias[:, s : s + 1])
                 else:
                     nc.scalar.activation(out=result[:, s, :], in_=y[s], func=ACT.Identity, bias=bias[:, s : s + 1])
-            nc.sync.dma_start(out=out[:, lo : lo + width].rearrange("(s p) j -> p s j", p=P), in_=result[:])
+            nc.sync.dma_start(
+                out=out[:, CHUNK * q : CHUNK * (q + 1)].rearrange("(s p) j -> p s j", p=P), in_=result[:]
+            )
 
-        PAIRS = ((0, 1), (2, 3))
-        ALL = (0, 1, 2, 3)
-
-        picked_a = [held([P, HALF], U32, "picked_a%d" % g) for g in range(LOOKS)]
-        for g in range(LOOKS):
-            pick_words(picked_a[g][:], g, 0)
-        for g in range(LOOKS):
-            part_words(picked_a[g], g, 0, held([P, PASSES, 2 * HALF], U8, "parted_a%d" % g))
-        cast_w(0, 0, 0, 64, "scalar")
-        cast_w(0, 1, 0, W0_SCALAR, "scalar")
-        cast_w(0, 1, W0_SCALAR, 64, "vector")
-        picked_b = [held([P, HALF], U32, "picked_b0")]
-        pick_words(picked_b[0][:], 0, 1)
-        quant_w(0)
-        pair_look = {}
-        for g in range(LOOKS):
-            for u in range(2):
-                pair_look[g, u] = bank([P, 2, HALF], "pair_look", 2 * u + g)
-                look(pair_look[g, u], PAIRS[u], g, 0, HALF, 0, True, False)
-        picked_b.append(placed([P, HALF], U32, "picked_b1", SLOTS["w_raw01"]))
-        pick_words(picked_b[1][:], 1, 1)
-        for g in range(LOOKS):
-            dst = placed([P, PASSES, 2 * HALF], U8, "parted_b%d" % g, SLOTS["w_raw01"], 1024 * (g + 1))
-            part_words(picked_b[g], g, 1, dst)
-        look2 = [bank([P, PACK, CHUNK], "look2", 4 + g) for g in range(LOOKS)]
-        look(look2[0], ALL, 0, 2 * CHUNK, CHUNK, 0, True, False)
-        cast_w(1, 0, 0, 64, "scalar")
-        cast_w(1, 1, 0, W1_SCALAR, "scalar")
-        cast_w(1, 1, W1_SCALAR, 64, "vector")
-        quant_w(1)
-        for g in range(LOOKS):
-            for u in range(2):
-                look(pair_look[g, u], PAIRS[u], g, 0, HALF, 1, False, True)
-
-        wide = PACK * CHUNK
-        c_bf = {(0, 0): placed([P, 2 * wide], BF16, "c_bf00", SLOTS["w_raw11"])}
-
-        def cast_chunk(a, q, engine):
-            h, k = divmod(q, 2)
-            cast_c(c_bf[a, h][:, wide * k : wide * (k + 1)], a, h, CHUNK * k, CHUNK, engine)
-
-        cast_chunk(0, 0, "vector")
-        cast_chunk(0, 1, "scalar")
-        wc_perm = placed([P, PASSES, 2 * R], U8, "wc_perm", SLOTS["w_raw11"], 2048)
-        nc.vector.tensor_copy(
-            out=wc_perm[:].bitcast(U16).rearrange("p a (t m) -> p a t m", t=PACK),
-            in_=wc_raw[:].bitcast(U16).rearrange("p a (m t) -> p a t m", t=PACK),
-        )
-
-        def copy_first(acc, name, relu):
-            first = held([P, acc.shape[2], acc.shape[1]], F32, name)
-            if relu:
-                nc.scalar.activation(out=first[:], in_=woven(acc), func=ACT.Relu)
-            else:
-                nc.scalar.copy(out=first[:], in_=woven(acc))
-            return first
-
-        def join(dst, acc, other, op):
-            nc.vector.tensor_tensor(out=dst, in0=woven(acc), in1=other[:], op=op)
-
-        def pooled(acc, first, name):
-            dst = held(list(first.shape), F32, name)
-            join(dst[:], acc, first, ALU.max)
-            return dst
-
-        c00 = quantised(c_bf[0, 0][:], "c00")
-        first_a = [copy_first(pair_look[0, u], "first_a%d" % u, False) for u in range(2)]
-        look(look2[0], ALL, 0, 2 * CHUNK, CHUNK, 1, False, True)
-        look(look2[1], ALL, 1, 2 * CHUNK, CHUNK, 1, True, False)
-        look(look2[1], ALL, 1, 2 * CHUNK, CHUNK, 0, False, True)
-        pooled_a = [pooled(pair_look[1, 0], first_a[0], "pooled_a0")]
-        c_bf[1, 0] = held([P, 2 * wide], BF16, "c_bf10", "parted_a0")
-        cast_chunk(1, 0, "vector")
-        cast_chunk(1, 1, "scalar")
-        pooled_a.append(pooled(pair_look[1, 1], first_a[1], "pooled_a1"))
-        own_a = [bank([P, 2, HALF], "own_a", 2 * u) for u in range(2)]
-        for u in range(2):
-            own(own_a[u], PAIRS[u], 0, c00, 0, HALF, True, False)
-        c10 = quantised(c_bf[1, 0][:], "c10")
-        for u in range(2):
-            own(own_a[u], PAIRS[u], 1, c10, 0, HALF, False, True)
-        joint = [bank([P, PACK, CHUNK], "joint", 6 + g) for g in range(LOOKS)]
-        for g in range(LOOKS):
-            look(joint[g], ALL, g, 3 * CHUNK, CHUNK, 1, True, False)
-            look(joint[g], ALL, g, 3 * CHUNK, CHUNK, 0, False, False)
-        first2 = copy_first(look2[0], "first2", False)
-        c_bf[0, 1] = placed([P, 2 * wide], BF16, "c_bf01", SLOTS["c_raw10"])
-        cast_chunk(0, 2, "vector")
-        cast_chunk(0, 3, "scalar")
-        pooled2 = pooled(look2[1], first2, "pooled2")
-        c01 = quantised(c_bf[0, 1][:], "c01")
-        own2 = bank([P, PACK, CHUNK], "own2", 4)
-        own(own2, ALL, 0, c01, 0, CHUNK, True, False)
-        own(joint[0], ALL, 0, c01, CHUNK, CHUNK, False, False)
-        summed_a = held([P, 2, HALF, 2], BF16, "summed_a")
-        join(summed_a[:, 0, :, :], own_a[0], pooled_a[0], ALU.add)
-        c_bf[1, 1] = placed([P, 2 * wide], BF16, "c_bf11", SLOTS["c_raw01"])
-        cast_chunk(1, 2, "scalar")
-        cast_chunk(1, 3, "scalar")
-        c12 = quantised(c_bf[1, 1][:, 0:wide], "c12")
-        own(own2, ALL, 1, c12, 0, CHUNK, False, True)
-        own(joint[1], ALL, 0, c01, CHUNK, CHUNK, False, False)
-        join(summed_a[:, 1, :, :], own_a[1], pooled_a[1], ALU.add)
-        c13 = quantised(c_bf[1, 1][:, wide : 2 * wide], "c13")
-        for g in range(LOOKS):
-            own(joint[g], ALL, 1, c13, 0, CHUNK, False, True)
-        summed2 = held([P, CHUNK, PACK], BF16, "summed2")
-        join(summed2[:], own2, pooled2, ALU.add)
-        hidden_a = placed([P, HALF * PACK], BF16, "hidden_a", SLOTS["c_raw11"])
-        nc.vector.tensor_scalar_max(
-            out=hidden_a[:].rearrange("p (j u e) -> p j u e", u=2, e=2),
-            in0=summed_a[:].rearrange("p u j e -> p j u e"),
-            scalar1=0.0,
-        )
-        hidden2 = held([P, CHUNK * PACK], BF16, "hidden2")
-        nc.vector.tensor_scalar_max(out=hidden2[:], in0=summed2[:].rearrange("p j t -> p (j t)"), scalar1=0.0)
-        h_a = quantised(hidden_a[:], "h_a")
-        first3 = copy_first(joint[0], "first3", True)
-        y_a = bank([P, N // P, HALF], "y_a", 1)
-        project(h_a, 0, HALF, [y_a[:, s, :] for s in range(N // P)], ("scalar", "scalar"), "result_a")
-        h2 = quantised(hidden2[:], "h2")
-        y2 = [bank([P, CHUNK], "y2", k)[:] for k in (0, 2)]
-        hidden3 = held([P, CHUNK, PACK], BF16, "hidden3")
-        join(hidden3[:], joint[1], first3, ALU.max)
-        h3 = quantised(hidden3[:].rearrange("p j t -> p (j t)"), "h3")
-        project(h2, 2 * CHUNK, CHUNK, y2, ("scalar", "vector"), "result2")
-        y3 = [bank([P, CHUNK], "y3", k)[:] for k in (3, 5)]
-        project(h3, 3 * CHUNK, CHUNK, y3, ("scalar", "vector"), "result3")
+        cast_c(0, 0, HALF, c_raw[0], 0, "vector")
+        cast_c(0, 2, CHUNK, c_raw[0], HALF, "vector", 0, HALF)
+        cast_c(0, 2, CHUNK, c_raw[0], HALF + CHUNK, "scalar", CHUNK)
+        deal_wc()
+        copy_first(0)
+        copy_first(1)
+        copy_first(2)
+        quant_c(0, 0)
+        passes(look_bank[0, LAST], look_operands(0, LAST, 1), False, False)
+        own(0, 0)
+        own(1, 0)
+        passes(look_bank[1, LAST], look_operands(1, LAST, 1), False, False)
+        pool_pair(0)
+        quant_c(0, 2)
+        pool_pair(1)
+        own(2, 0)
+        cast_c(1, 0, 128, c_raw[1, 0], 0, "scalar")
+        quant_c(1, 0)
+        own(0, 1)
+        own_joint(0, 0)
+        pool_pair(2)
+        cast_c(1, 1, 128, c_raw[1, 0], 128, "scalar")
+        quant_c(1, 1)
+        own(1, 1)
+        own_joint(1, 0)
+        add_own(0)
+        cast_c(1, 2, 128, c_raw[1, 1], 0, "scalar")
+        cast_c(1, 3, 128, c_raw[1, 1], 128, "scalar")
+        quant_c(1, 2)
+        quant_c(1, 3)
+        own(2, 1)
+        own_joint(0, 1)
+        own_joint(1, 1)
+        add_own(1)
+        relu(0)
+        add_own(2)
+        copy_first(3)
+        relu(1)
+        quant_h(0)
+        relu(2)
+        quant_h(1)
+        project(0)
+        project(1)
+        pool_pair(3)
+        quant_h(2)
+        quant_h(3)
+        project(2)
+        project(3)

@@ -28,7 +28,7 @@ ROWS = 32
 LOOK_AT, WC_AT, PLANE_W = 0, LOOKS * J, LOOKS * J + R
 
 W0_SCALAR = 64
-W1_SCALAR = 76
+W1_SCALAR = 80
 RAW = PACK * R * 4
 
 
@@ -150,21 +150,15 @@ def tile_list_pnet_bias_kernel(
         cast_w(0, 0, W0_SCALAR, "scalar")
         cast_w(0, W0_SCALAR, P, "vector")
         quant(w_codes[0][:], w_plane[0][:], w_bf[0][:])
-        pick_words(0, 0, CHUNK, 0)
-        pick_words(0, CHUNK, CHUNK, 2048 - 256)
-        part_words(0, 0, CHUNK)
-        part_words(0, CHUNK, CHUNK)
-        pick_words(0, HALF, HALF, 0)
-        pick_words(1, 0, HALF, 1024)
-        pick_words(1, HALF, HALF, 2048)
+        pick_words(0, 0, HALF, 0)
+        pick_words(0, HALF, HALF, 2048)
+        part_words(0, 0, HALF)
+        pick_words(1, 0, J, 0)
         part_words(0, HALF, HALF)
-        part_words(1, 0, HALF)
-        part_words(1, HALF, HALF)
         cast_w(1, 0, W1_SCALAR, "scalar")
         cast_w(1, W1_SCALAR, P, "vector")
-        for u in range(2):
-            cols = slice(2 * P * u, 2 * P * (u + 1))
-            quant(w_codes[1][:, cols], w_plane[1][:, cols], w_bf[1][:, PACK * cols.start : PACK * cols.stop])
+        part_words(1, 0, J)
+        quant(w_codes[1][:], w_plane[1][:], w_bf[1][:])
         wc_perm = placed([P, PASSES, 2 * R], U8, "wc_perm", RAW + 4096)
 
         def deal_wc():
@@ -175,13 +169,10 @@ def tile_list_pnet_bias_kernel(
 
         c_bf, c_codes, c_plane = {}, {}, {}
 
-        def cast_c(a, q, width, raw, lo, engine, at=0, whole=None):
-            shape, name = [P, PACK * (whole or width)], "c_bf%d%d" % (a, q)
-            if at == 0 and a == 0:
-                c_bf[a, q] = placed(shape, BF16, name, RAW + 1024 * q)
-            elif at == 0:
-                c_bf[a, q] = held(shape, BF16, name)
-            dst = c_bf[a, q][:, PACK * at : PACK * (at + width)].rearrange("p (n e i) -> p n i e", e=4, i=PACK)
+        def cast_c(a, q, width, raw, lo, engine):
+            shape, name = [P, PACK * width], "c_bf%d%d" % (a, q)
+            c_bf[a, q] = placed(shape, BF16, name, RAW) if a == 0 else held(shape, BF16, name)
+            dst = c_bf[a, q][:].rearrange("p (n e i) -> p n i e", e=4, i=PACK)
             src = raw[:, :, lo : lo + width].rearrange("p i (n e) -> p n i e", e=4)
             round_copy(engine, dst, src)
 
@@ -238,9 +229,11 @@ def tile_list_pnet_bias_kernel(
         for g in range(LOOKS):
             for q in range(CHUNKS):
                 passes(look_bank[g, q], look_operands(g, q, 0), True, False)
-        for q in range(LAST):
-            for g in range(LOOKS):
+        for g in range(LOOKS):
+            for q in range(LAST):
                 passes(look_bank[g, q], look_operands(g, q, 1), False, True)
+        for g in range(LOOKS):
+            passes(look_bank[g, LAST], look_operands(g, LAST, 1), False, False)
 
         first, pooled, own_bank, summed, hidden, h_codes, h_plane = {}, {}, {}, {}, {}, {}, {}
 
@@ -314,22 +307,17 @@ def tile_list_pnet_bias_kernel(
                 out=out[:, CHUNK * q : CHUNK * (q + 1)].rearrange("(s p) j -> p s j", p=P), in_=result[:]
             )
 
-        cast_c(0, 0, HALF, c_raw[0], 0, "vector")
-        cast_c(0, 2, CHUNK, c_raw[0], HALF, "vector", 0, HALF)
-        cast_c(0, 2, CHUNK, c_raw[0], HALF + CHUNK, "scalar", CHUNK)
+        cast_c(0, 0, J, c_raw[0], 0, "vector")
         deal_wc()
         copy_first(0)
         copy_first(1)
         copy_first(2)
         quant_c(0, 0)
-        passes(look_bank[0, LAST], look_operands(0, LAST, 1), False, False)
         own(0, 0)
         own(1, 0)
-        passes(look_bank[1, LAST], look_operands(1, LAST, 1), False, False)
-        pool_pair(0)
-        quant_c(0, 2)
-        pool_pair(1)
         own(2, 0)
+        pool_pair(0)
+        pool_pair(1)
         cast_c(1, 0, 128, c_raw[1, 0], 0, "scalar")
         quant_c(1, 0)
         own(0, 1)

@@ -27,8 +27,6 @@ HALF = 2 * CHUNK
 ROWS = 32
 LOOK_AT, WC_AT, PLANE_W = 0, LOOKS * J, LOOKS * J + R
 
-W0_SCALAR = 64
-W1_SCALAR = 80
 RAW = PACK * R * 4
 
 
@@ -73,9 +71,9 @@ def tile_list_pnet_bias_kernel(
             nc.sync.dma_start(out=raw[:], in_=rows.rearrange("(p i) n -> p i n", i=PACK))
             return raw
 
-        w_raw = {0: load_rows(w, 0, 0, R, "w_raw0", 0)}
         table = held([P, T], I32, "table")
         nc.sync.dma_start(out=table[:], in_=tab_words[0].rearrange("p t b -> p (t b)").bitcast(I32))
+        w_raw = {0: load_rows(w, 0, 0, R, "w_raw0", 0)}
 
         picked_rows = held([P, LOOKS * J], U8, "picked_rows")
         nc.vector.tensor_copy(out=picked_rows[:], in_=tab_rows[:].indirect(offsets[:]))
@@ -111,7 +109,7 @@ def tile_list_pnet_bias_kernel(
         with nc.allow_non_contiguous_dma(reason="one bias value a partition"):
             nc.sync.dma_start(out=bias[:], in_=b.rearrange("(s p) -> p s", p=P))
 
-        w_bf = [held([P, PACK * R], BF16, "w_bf%d" % a) for a in range(PASSES)]
+        w_bf = {(a, u): held([P, 2 * PACK * P], BF16, "w_bf%d%d" % (a, u)) for a in range(PASSES) for u in range(2)}
         w_codes = [held([P, R], U32, "w_codes%d" % a) for a in range(PASSES)]
         w_plane = [held([P, R], U8, "w_plane%d" % a) for a in range(PASSES)]
 
@@ -121,25 +119,29 @@ def tile_list_pnet_bias_kernel(
             else:
                 nc.scalar.copy(out=dst, in_=src)
 
-        def cast_w(a, lo, hi, engine):
-            dst = w_bf[a][:].rearrange("p (t m i) -> p m i t", t=PACK, i=PACK)[:, lo:hi, :, :]
-            src = w_raw[a][:].rearrange("p i (m t) -> p m i t", t=PACK)[:, lo:hi, :, :]
+        def cast_w(a, u, engine):
+            dst = w_bf[a, u][:].rearrange("p (e m i) -> p m i e", e=2, i=PACK)
+            src = w_raw[a][:].rearrange("p i (m u e) -> p u m i e", u=2, e=2)[:, u, :, :, :]
             round_copy(engine, dst, src)
+
+        def quant_w(a, u):
+            cols = slice(2 * P * u, 2 * P * (u + 1))
+            quant(w_codes[a][:, cols], w_plane[a][:, cols], w_bf[a, u][:])
 
         def quant(codes, scales, src):
             nc.vector.quantize_mx(out=codes.bitcast(FP8X4), scales=scales, in_=src)
 
         picked, look_words = {}, {}
 
-        def pick_words(g, lo, width, at):
-            picked[g, lo] = placed([P, width], U32, "picked%d_%d" % (g, lo), at)
+        def pick_words(g, lo, width):
+            picked[g, lo] = held([P, width], U32, "picked%d_%d" % (g, lo))
             at = (g * J + lo) // 16
             nc.vector.tensor_copy(
                 out=picked[g, lo][:], in_=table[:].bitcast(U32).indirect(offsets[:, at : at + width // 16])
             )
 
-        def part_words(g, lo, width):
-            parted = held([P, PASSES, 2 * width], U8, "parted%d_%d" % (g, lo))
+        def part_words(g, lo, width, tag=None):
+            parted = held([P, PASSES, 2 * width], U8, "parted%d_%d" % (g, lo), tag)
             nc.vector.tensor_copy(
                 out=parted[:].bitcast(U16),
                 in_=picked[g, lo][:].bitcast(U16).rearrange("p (j d) -> p d j", d=PASSES),
@@ -147,18 +149,18 @@ def tile_list_pnet_bias_kernel(
             for part in range(width // CHUNK):
                 look_words[g, lo // CHUNK + part] = parted[:, :, 2 * CHUNK * part : 2 * CHUNK * (part + 1)]
 
-        cast_w(0, 0, W0_SCALAR, "scalar")
-        cast_w(0, W0_SCALAR, P, "vector")
-        quant(w_codes[0][:], w_plane[0][:], w_bf[0][:])
-        pick_words(0, 0, HALF, 0)
-        pick_words(0, HALF, HALF, 2048)
-        part_words(0, 0, HALF)
-        pick_words(1, 0, J, 0)
-        part_words(0, HALF, HALF)
-        cast_w(1, 0, W1_SCALAR, "scalar")
-        cast_w(1, W1_SCALAR, P, "vector")
-        part_words(1, 0, J)
-        quant(w_codes[1][:], w_plane[1][:], w_bf[1][:])
+        pick_words(0, 0, J)
+        pick_words(1, 0, J)
+        part_words(0, 0, J)
+        cast_w(0, 0, "scalar")
+        quant_w(0, 0)
+        part_words(1, 0, J, "w_bf00")
+        cast_w(0, 1, "scalar")
+        quant_w(0, 1)
+        cast_w(1, 0, "scalar")
+        cast_w(1, 1, "vector")
+        quant_w(1, 1)
+        quant_w(1, 0)
         wc_perm = placed([P, PASSES, 2 * R], U8, "wc_perm", RAW + 4096)
 
         def deal_wc():
@@ -169,10 +171,12 @@ def tile_list_pnet_bias_kernel(
 
         c_bf, c_codes, c_plane = {}, {}, {}
 
-        def cast_c(a, q, width, raw, lo, engine):
-            shape, name = [P, PACK * width], "c_bf%d%d" % (a, q)
-            c_bf[a, q] = placed(shape, BF16, name, RAW) if a == 0 else held(shape, BF16, name)
-            dst = c_bf[a, q][:].rearrange("p (n e i) -> p n i e", e=4, i=PACK)
+        def cast_c(a, q, width, raw, lo, engine, whole=None):
+            if (a, q) not in c_bf:
+                shape, name = [P, PACK * (whole or width)], "c_bf%d%d" % (a, q)
+                c_bf[a, q] = placed(shape, BF16, name, RAW) if a == 0 else held(shape, BF16, name)
+            at = lo if a == 0 else 0
+            dst = c_bf[a, q][:, PACK * at : PACK * (at + width)].rearrange("p (n e i) -> p n i e", e=4, i=PACK)
             src = raw[:, :, lo : lo + width].rearrange("p i (n e) -> p n i e", e=4)
             round_copy(engine, dst, src)
 
@@ -186,8 +190,8 @@ def tile_list_pnet_bias_kernel(
                 c_codes[a, q + part] = codes[:, cols]
                 c_plane[a, q + part] = scales[:, cols]
 
-        def passes(bank, operands, start, stop):
-            for t in range(PACK):
+        def passes(bank, operands, start, stop, slices=range(PACK)):
+            for t in slices:
                 lhsT, lhsT_scale, rhs, rhs_scale = operands(t)
                 nc.tensor.matmul_mx(
                     out=bank[:, t, :],
@@ -195,8 +199,8 @@ def tile_list_pnet_bias_kernel(
                     lhsT_scale=lhsT_scale,
                     rhs=rhs,
                     rhs_scale=rhs_scale,
-                    start=(start and t == 0),
-                    stop=(stop and t == PACK - 1),
+                    start=(start and t == slices[0]),
+                    stop=(stop and t == slices[-1]),
                 )
 
         def look_operands(g, q, a):
@@ -226,14 +230,15 @@ def tile_list_pnet_bias_kernel(
         for g in range(LOOKS):
             for q in range(CHUNKS):
                 look_bank[g, q] = bank_tile([P, PACK, CHUNK], "look_bank", g, q)
-        for g in range(LOOKS):
-            for q in range(CHUNKS):
-                passes(look_bank[g, q], look_operands(g, q, 0), True, False)
-        for g in range(LOOKS):
-            for q in range(LAST):
-                passes(look_bank[g, q], look_operands(g, q, 1), False, True)
-        for g in range(LOOKS):
-            passes(look_bank[g, LAST], look_operands(g, LAST, 1), False, False)
+        for a, u in ((0, 0), (0, 1), (1, 1), (1, 0)):
+            for g in range(LOOKS):
+                for q in range(2):
+                    first_pass, last_pass = (a, u) == (0, 0), (a, u) == (1, 0)
+                    passes(look_bank[g, q], look_operands(g, q, a), first_pass, last_pass, (2 * u, 2 * u + 1))
+        for q in range(2, CHUNKS):
+            for g in range(LOOKS):
+                passes(look_bank[g, q], look_operands(g, q, 1), True, False)
+                passes(look_bank[g, q], look_operands(g, q, 0), False, q != LAST)
 
         first, pooled, own_bank, summed, hidden, h_codes, h_plane = {}, {}, {}, {}, {}, {}, {}
 
@@ -307,16 +312,17 @@ def tile_list_pnet_bias_kernel(
                 out=out[:, CHUNK * q : CHUNK * (q + 1)].rearrange("(s p) j -> p s j", p=P), in_=result[:]
             )
 
-        cast_c(0, 0, J, c_raw[0], 0, "vector")
+        cast_c(0, 0, 3 * CHUNK, c_raw[0], 0, "vector", J)
         deal_wc()
         copy_first(0)
         copy_first(1)
+        cast_c(0, 0, CHUNK, c_raw[0], 3 * CHUNK, "scalar")
         copy_first(2)
+        pool_pair(0)
         quant_c(0, 0)
         own(0, 0)
         own(1, 0)
         own(2, 0)
-        pool_pair(0)
         pool_pair(1)
         cast_c(1, 0, 128, c_raw[1, 0], 0, "scalar")
         quant_c(1, 0)

from contextlib import ExitStack

import concourse.mybir as mybir

K, R, N, T, J = 1024, 512, 256, 2048, 512
FLOPS = 2 * (3 * K * R * J + R * N * J)

F32 = mybir.dt.float32
BF16 = mybir.dt.bfloat16
I32 = mybir.dt.int32
U32 = mybir.dt.uint32
U16 = mybir.dt.uint16
U8 = mybir.dt.uint8
FP8X4 = mybir.dt.float8_e4m3fn_x4
FP4X4 = mybir.dt.float4_e2m1fn_x4
ALU = mybir.AluOpType
ACT = mybir.ActivationFunctionType

P = 128
PACK = 4
PASSES = K // (P * PACK)
LOOKS = 2
CHUNK = 128
CHUNKS = J // CHUNK
LAST = CHUNKS - 1
HALF = 2 * CHUNK
ROWS = 32
LOOK_AT, WC_AT, PLANE_W = 0, LOOKS * J, LOOKS * J + R

RAW = PACK * R * 4


def tile_list_pnet_bias_kernel(
    tc, tab_words, tab_scales, c, w, wc_words, wc_scales, wd_words, wd_scales, b, offs, out
):
    nc = tc.nc
    with ExitStack() as ctx:
        keep = ctx.enter_context(tc.tile_pool(name="keep", bufs=1))
        shared = ctx.enter_context(tc.tile_pool(name="shared", bufs=1))
        psum = ctx.enter_context(tc.psum_pool(name="psum", bufs=1))

        def held(shape, dtype, name, tag=None):
            return keep.tile(shape, dtype, name=name, tag=tag or name, align_bytes=64)

        def placed(shape, dtype, name, at):
            return shared.tile(shape, dtype, name=name, tag=name, align_bytes=64, offset=at)

        offsets = keep.tile([P, LOOKS * J // 16], U16, name="offsets")
        nc.sync.dma_start(offsets[:], offs)

        tab_rows = held([P, T], U8, "tab_rows")
        wc_rows = held([P, R], U8, "wc_rows")
        stage = held([P, PLANE_W], U8, "stage")
        plane = held([P, PASSES, PLANE_W], U8, "plane")
        nc.sync.dma_start(
            out=tab_rows[0:ROWS, :].bitcast(I32), in_=tab_scales.bitcast(I32).rearrange("a q t -> q a t")
        )
        nc.sync.dma_start(
            out=wc_rows[0:ROWS, :].bitcast(I32), in_=wc_scales.bitcast(I32).rearrange("a q t -> q a t")
        )
        nc.gpsimd.memset(wc_rows[32:64, :].bitcast(I32), 0)
        nc.gpsimd.memset(tab_rows[32:64, :].bitcast(I32), 0)
        nc.vector.memset(wc_rows[64:128, :].bitcast(I32), 0)
        nc.vector.memset(tab_rows[64:128, :].bitcast(I32), 0)
        nc.vector.memset(plane[:].rearrange("p a j -> p (a j)").bitcast(I32), 0)

        def load_rows(src, a, lo, hi, name, at=None):
            shape = [P, PACK, hi - lo]
            raw = held(shape, F32, name) if at is None else placed(shape, F32, name, at)
            rows = src[512 * a : 512 * (a + 1), lo:hi]
            nc.sync.dma_start(out=raw[:], in_=rows.rearrange("(p i) n -> p i n", i=PACK))
            return raw

        table = held([P, T], I32, "table")
        nc.sync.dma_start(out=table[:], in_=tab_words[0].rearrange("p t b -> p (t b)").bitcast(I32))
        w_raw = {0: load_rows(w, 0, 0, R, "w_raw0", 0)}

        picked_rows = held([P, LOOKS * J], U8, "picked_rows")
        nc.vector.tensor_copy(out=picked_rows[:], in_=tab_rows[:].indirect(offsets[:]))
        nc.vector.tensor_copy(
            out=stage[:, WC_AT:PLANE_W].rearrange("p (t m) -> p t m", t=PACK),
            in_=wc_rows[:].rearrange("p (m t) -> p t m", t=PACK),
        )
        nc.vector.tensor_copy(
            out=stage[0:ROWS, LOOK_AT:WC_AT].bitcast(I32), in_=picked_rows[0:ROWS, :].bitcast(I32)
        )
        for q in range(4):
            nc.sync.dma_start(
                out=plane[32 * q : 32 * q + 4, :, :].bitcast(I32),
                in_=stage[8 * q : 8 * q + 8, :].bitcast(I32),
            )

        w_raw[1] = load_rows(w, 1, 0, R, "w_raw1", RAW)
        c_raw = {0: load_rows(c, 0, 0, J, "c_raw0")}
        wc_raw = held([P, PASSES, 2 * R], U8, "wc_raw")
        nc.sync.dma_start(out=wc_raw[:].bitcast(I32), in_=wc_words.bitcast(I32).rearrange("a p n -> p a n"))
        c_raw[1, 0] = load_rows(c, 1, 0, HALF, "c_raw1a")
        c_raw[1, 1] = load_rows(c, 1, HALF, J, "c_raw1b")
        wd_raw = held([P, 2 * N], U8, "wd_raw")
        nc.sync.dma_start(out=wd_raw[:].bitcast(I32), in_=wd_words[0].bitcast(I32))
        wd_plane = held([P, N], U8, "wd_plane")
        nc.gpsimd.memset(wd_plane[:].bitcast(I32), 0)
        for q in range(4):
            nc.sync.dma_start(
                out=wd_plane[32 * q : 32 * q + 4, :].bitcast(I32),
                in_=wd_scales[0, 4 * q : 4 * q + 4, :].bitcast(I32),
            )
        bias = held([P, N // P], F32, "bias")
        with nc.allow_non_contiguous_dma(reason="one bias value a partition"):
            nc.sync.dma_start(out=bias[:], in_=b.rearrange("(s p) -> p s", p=P))

        w_bf = {(a, u): held([P, 2 * PACK * P], BF16, "w_bf%d%d" % (a, u)) for a in range(PASSES) for u in range(2)}
        w_codes = [held([P, R], U32, "w_codes%d" % a) for a in range(PASSES)]
        w_plane = [held([P, R], U8, "w_plane%d" % a) for a in range(PASSES)]

        def round_copy(engine, dst, src):
            if engine == "vector":
                nc.vector.tensor_copy(out=dst, in_=src)
            else:
                nc.scalar.copy(out=dst, in_=src)

        def cast_w(a, u, engine):
            dst = w_bf[a, u][:].rearrange("p (e m i) -> p m i e", e=2, i=PACK)
            src = w_raw[a][:].rearrange("p i (m u e) -> p u m i e", u=2, e=2)[:, u, :, :, :]
            round_copy(engine, dst, src)

        def quant_w(a, u):
            cols = slice(2 * P * u, 2 * P * (u + 1))
            quant(w_codes[a][:, cols], w_plane[a][:, cols], w_bf[a, u][:])

        def quant(codes, scales, src):
            nc.vector.quantize_mx(out=codes.bitcast(FP8X4), scales=scales, in_=src)

        picked, look_words = {}, {}

        def pick_words(g, lo, width):
            picked[g, lo] = held([P, width], U32, "picked%d_%d" % (g, lo))
            at = (g * J + lo) // 16
            nc.vector.tensor_copy(
                out=picked[g, lo][:], in_=table[:].bitcast(U32).indirect(offsets[:, at : at + width // 16])
            )

        def part_words(g, lo, width, tag=None):
            parted = held([P, PASSES, 2 * width], U8, "parted%d_%d" % (g, lo), tag)
            nc.vector.tensor_copy(
                out=parted[:].bitcast(U16),
                in_=picked[g, lo][:].bitcast(U16).rearrange("p (j d) -> p d j", d=PASSES),
            )
            for part in range(width // CHUNK):
                look_words[g, lo // CHUNK + part] = parted[:, :, 2 * CHUNK * part : 2 * CHUNK * (part + 1)]

        pick_words(0, 0, J)
        pick_words(1, 0, J)
        part_words(0, 0, J)
        cast_w(0, 0, "scalar")
        quant_w(0, 0)
        part_words(1, 0, J, "w_bf00")
        cast_w(0, 1, "scalar")
        quant_w(0, 1)
        cast_w(1, 0, "scalar")
        cast_w(1, 1, "vector")
        quant_w(1, 1)
        quant_w(1, 0)
        wc_perm = placed([P, PASSES, 2 * R], U8, "wc_perm", RAW + 4096)

        def deal_wc():
            nc.vector.tensor_copy(
                out=wc_perm[:].bitcast(U16).rearrange("p a (t m) -> p a t m", t=PACK),
                in_=wc_raw[:].bitcast(U16).rearrange("p a (m t) -> p a t m", t=PACK),
            )

        c_bf, c_codes, c_plane = {}, {}, {}

        def cast_c(a, q, width, raw, lo, engine, whole=None):
            if (a, q) not in c_bf:
                shape, name = [P, PACK * (whole or width)], "c_bf%d%d" % (a, q)
                c_bf[a, q] = placed(shape, BF16, name, RAW) if a == 0 else held(shape, BF16, name)
            at = lo if a == 0 else 0
            dst = c_bf[a, q][:, PACK * at : PACK * (at + width)].rearrange("p (n e i) -> p n i e", e=4, i=PACK)
            src = raw[:, :, lo : lo + width].rearrange("p i (n e) -> p n i e", e=4)
            round_copy(engine, dst, src)

        def quant_c(a, q):
            width = c_bf[a, q].shape[1] // PACK
            codes = held([P, width], U32, "c_codes%d%d" % (a, q))
            scales = held([P, width], U8, "c_plane%d%d" % (a, q))
            quant(codes[:], scales[:], c_bf[a, q][:])
            for part in range(width // CHUNK):
                cols = slice(CHUNK * part, CHUNK * (part + 1))
                c_codes[a, q + part] = codes[:, cols]
                c_plane[a, q + part] = scales[:, cols]

        def passes(bank, operands, start, stop, slices=range(PACK)):
            for t in slices:
                lhsT, lhsT_scale, rhs, rhs_scale = operands(t)
                nc.tensor.matmul_mx(
                    out=bank[:, t, :],
                    lhsT=lhsT,
                    lhsT_scale=lhsT_scale,
                    rhs=rhs,
                    rhs_scale=rhs_scale,
                    start=(start and t == slices[0]),
                    stop=(stop and t == slices[-1]),
                )

        def look_operands(g, q, a):
            at = LOOK_AT + J * g + CHUNK * q
            return lambda t: (
                w_codes[a][:, P * t : P * (t + 1)].bitcast(FP8X4),
                w_plane[a][:, P * t : P * (t + 1)],
                look_words[g, q][:, a, :].bitcast(FP4X4),
                plane[:, a, at : at + CHUNK],
            )

        def own_operands(q, a):
            return lambda t: (
                wc_perm[:, a, 2 * P * t : 2 * P * (t + 1)].bitcast(FP4X4),
                plane[:, a, WC_AT + P * t : WC_AT + P * (t + 1)],
                c_codes[a, q].bitcast(FP8X4),
                c_plane[a, q],
            )

        def bank_tile(shape, name, g, q):
            return psum.tile(shape, F32, name=name, tag="bank%d%d" % (g, q))

        def woven(bank):
            return bank[:].rearrange("p t j -> p j t")

        look_bank = {}
        for g in range(LOOKS):
            for q in range(CHUNKS):
                look_bank[g, q] = bank_tile([P, PACK, CHUNK], "look_bank", g, q)
        for a, u in ((0, 0), (0, 1), (1, 1), (1, 0)):
            for g in range(LOOKS):
                for q in range(2):
                    first_pass, last_pass = (a, u) == (0, 0), (a, u) == (1, 0)
                    passes(look_bank[g, q], look_operands(g, q, a), first_pass, last_pass, (2 * u, 2 * u + 1))
        for q in range(2, CHUNKS):
            for g in range(LOOKS):
                passes(look_bank[g, q], look_operands(g, q, 1), True, False)
                passes(look_bank[g, q], look_operands(g, q, 0), False, q != LAST)

        first, pooled, own_bank, summed, hidden, h_codes, h_plane = {}, {}, {}, {}, {}, {}, {}

        def copy_first(q):
            first[q] = held([P, CHUNK, PACK], F32, "first%d" % q)
            if q == LAST:
                nc.scalar.activation(out=first[q][:], in_=woven(look_bank[0, q]), func=ACT.Relu)
            else:
                nc.scalar.copy(out=first[q][:], in_=woven(look_bank[0, q]))

        def pool_pair(q):
            if q == LAST:
                hidden[q] = held([P, CHUNK * PACK], BF16, "hidden%d" % q)
                dst = hidden[q][:].rearrange("p (j t) -> p j t", t=PACK)
            else:
                pooled[q] = held([P, CHUNK, PACK], F32, "pooled%d" % q)
                dst = pooled[q][:]
            nc.vector.tensor_tensor(out=dst, in0=woven(look_bank[1, q]), in1=first[q][:], op=ALU.max)

        def own(q, a):
            if a == 0:
                own_bank[q] = bank_tile([P, PACK, CHUNK], "own_bank", 0, q)
            passes(own_bank[q], own_operands(q, a), a == 0, a == PASSES - 1)

        def own_joint(g, a):
            passes(look_bank[g, LAST], own_operands(LAST, a), False, a == PASSES - 1)

        def add_own(q):
            summed[q] = held([P, CHUNK, PACK], BF16, "summed%d" % q)
            nc.vector.tensor_tensor(out=summed[q][:], in0=woven(own_bank[q]), in1=pooled[q][:], op=ALU.add)

        def relu(q):
            hidden[q] = held([P, CHUNK * PACK], BF16, "hidden%d" % q)
            flat = summed[q][:].rearrange("p j t -> p (j t)")
            if q in (0,):
                nc.scalar.activation(out=hidden[q][:], in_=flat, func=ACT.Relu)
            else:
                nc.vector.tensor_scalar_max(out=hidden[q][:], in0=flat, scalar1=0.0)

        def quant_h(q):
            h_codes[q] = held([P, CHUNK], U32, "h_codes%d" % q)
            h_plane[q] = held([P, CHUNK], U8, "h_plane%d" % q)
            quant(h_codes[q][:], h_plane[q][:], hidden[q][:])

        Y_SLOTS = {2: ((1, 2), (0, 0)), 3: ((0, 1), (0, 2))}

        def project(q):
            shared = q in Y_SLOTS
            result = held([P, N // P, CHUNK], F32, "result%d" % q)
            if shared:
                y = [bank_tile([P, CHUNK], "y_bank", *slot)[:] for slot in Y_SLOTS[q]]
            else:
                y_bank = bank_tile([P, N // P, CHUNK], "y_bank", 1, q)
                y = [y_bank[:, s, :] for s in range(N // P)]
            for s in range(N // P):
                nc.tensor.matmul_mx(
                    out=y[s],
                    lhsT=wd_raw[:, 2 * P * s : 2 * P * (s + 1)].bitcast(FP4X4),
                    lhsT_scale=wd_plane[:, P * s : P * (s + 1)],
                    rhs=h_codes[q][:].bitcast(FP8X4),
                    rhs_scale=h_plane[q][:],
                    start=True,
                    stop=True,
                )
            for s in range(N // P):
                if shared and s == 1:
                    nc.vector.tensor_scalar_add(out=result[:, s, :], in0=y[s], scalar1=bias[:, s : s + 1])
                else:
                    nc.scalar.activation(out=result[:, s, :], in_=y[s], func=ACT.Identity, bias=bias[:, s : s + 1])
            nc.sync.dma_start(
                out=out[:, CHUNK * q : CHUNK * (q + 1)].rearrange("(s p) j -> p s j", p=P), in_=result[:]
            )

        cast_c(0, 0, 3 * CHUNK, c_raw[0], 0, "vector", J)
        deal_wc()
        copy_first(0)
        copy_first(1)
        cast_c(0, 0, CHUNK, c_raw[0], 3 * CHUNK, "scalar")
        copy_first(2)
        pool_pair(0)
        quant_c(0, 0)
        own(0, 0)
        own(1, 0)
        own(2, 0)
        pool_pair(1)
        cast_c(1, 0, 128, c_raw[1, 0], 0, "scalar")
        quant_c(1, 0)
        own(0, 1)
        own_joint(0, 0)
        pool_pair(2)
        cast_c(1, 1, 128, c_raw[1, 0], 128, "scalar")
        quant_c(1, 1)
        own(1, 1)
        own_joint(1, 0)
        add_own(0)
        cast_c(1, 2, 128, c_raw[1, 1], 0, "scalar")
        cast_c(1, 3, 128, c_raw[1, 1], 128, "scalar")
        quant_c(1, 2)
        quant_c(1, 3)
        own(2, 1)
        own_joint(0, 1)
        own_joint(1, 1)
        add_own(1)
        relu(0)
        add_own(2)
        copy_first(3)
        relu(1)
        quant_h(0)
        relu(2)
        quant_h(1)
        project(0)
        project(1)
        pool_pair(3)
        quant_h(2)
        quant_h(3)
        project(2)
        project(3)
